import numpy as np
import ml_dtypes


def mxq(x, axis, fmt="e4m3"):
    dtype, down = {"e4m3": (ml_dtypes.float8_e4m3fn, 7), "e5m2": (ml_dtypes.float8_e5m2, 14)}[fmt]
    v = np.moveaxis(np.asarray(x, np.float32).astype(ml_dtypes.bfloat16).astype(np.float64), axis, -1)
    blocks = v.reshape(v.shape[:-1] + (-1, 32))
    amax = np.abs(blocks).max(-1, keepdims=True)
    byte = np.maximum(np.where(amax > 0, np.frexp(amax)[1] - 1 + 127, 0) - down, 1)
    scale = np.exp2(byte - 127.0)
    codes = (blocks / scale).astype(np.float32).astype(dtype).astype(np.float64)
    return np.moveaxis((codes * scale).reshape(v.shape), -1, axis)


WIDE = False


def mx_kscale(k):
    if not WIDE:
        return np.ones(k)
    levels = np.array([10, -10, 5, -5, 0])
    if k % 512:
        return np.exp2(np.random.permutation(np.resize(levels, k // 32))).repeat(32)
    a = np.empty((k // 512, 16))
    for p in range(k // 512):
        a[p, :8] = np.random.permutation(np.resize(levels, 8))
        for g in range(8):
            far = levels[np.abs(levels - a[p, g]) >= 10]
            a[p, g + 8] = far[np.random.randint(len(far))]
    return np.exp2(a.ravel()).repeat(32)


def f64(x):
    return np.asarray(x).astype(np.float64)


def striped(idx):
    return np.tile(np.asarray(idx).reshape(-1, 16).T, (8, 1)).astype(np.uint16)


def unstriped(offs):
    return offs[:16].T.reshape(-1).astype(np.int64)


def striped8(idx):
    return np.asarray(idx).reshape(8, -1, 16).transpose(0, 2, 1).reshape(128, -1).astype(np.uint16)


def unstriped8(offs):
    return offs.reshape(8, 16, -1).transpose(0, 2, 1).reshape(8, -1).astype(np.int64)


def pick8(x, idx, run):
    r = np.arange(len(x))
    return x[r[:, None], idx[r % (8 * run) // run]]


E2M1 = np.array([0.0, 0.5, 1.0, 1.5, 2.0, 3.0, 4.0, 6.0, -0.0, -0.5, -1.0, -1.5, -2.0, -3.0, -4.0, -6.0])


def pack_weight(w, fmt):
    k, n = w.shape
    w = f64(np.asarray(w, np.float32).astype(ml_dtypes.bfloat16)).reshape(k // 32, 32, n)
    amax = np.abs(w).max(1)
    if fmt == "e4m3":
        byte = np.frexp(amax)[1] - 1 + 127 - 7
    else:
        mant, ex = np.frexp(amax / 6.0)
        byte = np.where(mant > 0.5, ex, ex - 1) + 127
    byte = np.clip(np.where(amax > 0, byte, 1), 1, 254)
    scaled = (w * np.exp2(127.0 - byte)[:, None, :]).reshape(k, n).astype(np.float32)
    by_word = np.ascontiguousarray(scaled.reshape(k // 512, 128, 4, n).transpose(0, 1, 3, 2))
    if fmt == "e4m3":
        words = by_word.astype(ml_dtypes.float8_e4m3fn).view(np.uint8)
    else:
        c = by_word.astype(ml_dtypes.float4_e2m1fn).view(np.uint8) & 0xF
        words = (c[..., 0::2] | (c[..., 1::2] << 4)).reshape(k // 512, 128, 2 * n)
    return np.ascontiguousarray(words), np.ascontiguousarray(byte.astype(np.uint8).reshape(k // 512, 16, n))


def unpack_weight(words, scales, fmt):
    g, _, n = scales.shape
    words = np.ascontiguousarray(words).reshape(g, 128, n, -1)
    if fmt == "e4m3":
        vals = words.view(ml_dtypes.float8_e4m3fn).astype(np.float64)
    else:
        nib = np.empty((g, 128, n, 4), np.uint8)
        nib[..., 0::2] = words & 0xF
        nib[..., 1::2] = words >> 4
        vals = E2M1[nib]
    vals = vals * np.repeat(np.exp2(scales.astype(np.float64) - 127.0), 8, axis=1)[..., None]
    return vals.transpose(0, 1, 3, 2).reshape(g * 512, n)


K, U, I, T, E = 512, 2048, 512, 1024, 512


def setup_inputs():
    n = np.random.standard_normal
    idx = np.random.permutation(U)[:I]
    idx2 = np.stack([np.random.permutation(T)[:I] for _ in range(8)])
    fk = mx_kscale(K)
    embp = pack_weight(n((K, U)) / fk[:, None], "e2m1")
    return {
        "emb_words": embp[0],
        "emb_scales": embp[1],
        "wv": (n((K, E)) * 1 / np.sqrt(K) * fk[:, None]).astype(np.float32),
        "old": (n((E, T))).astype(np.float32),
        "retain": (np.random.uniform(0.0, 1.0, (1, T))).astype(np.float32),
        "offs": striped(idx),
        "offs2": striped8(idx2),
    }


def reference(emb_words, emb_scales, wv, old, retain, offs, offs2):
    idx = unstriped(offs)
    idx2 = unstriped8(offs2)
    embu = unpack_weight(emb_words, emb_scales, "e2m1")
    wvq = mxq(f64(wv), 0, "e4m3")
    embidxg = embu[:, idx]
    v = wvq.T @ embidxg
    vf = np.zeros((E, T))
    vf[np.arange(E)[:, None], idx2[np.arange(E) % 512 // 64]] = v
    y = f64(old) * f64(retain) + vf
    return y

@@ -1,0 +1,156 @@
+from contextlib import ExitStack
+
+import concourse.mybir as mybir
+from concourse.masks import make_identity
+
+K, U, I, T, E = 512, 2048, 512, 1024, 512
+FLOPS = 2 * K * E * I
+
+F32 = mybir.dt.float32
+BF16 = mybir.dt.bfloat16
+I32 = mybir.dt.int32
+U32 = mybir.dt.uint32
+U16 = mybir.dt.uint16
+U8 = mybir.dt.uint8
+FP8X4 = mybir.dt.float8_e4m3fn_x4
+FP4X4 = mybir.dt.float4_e2m1fn_x4
+COPY = mybir.ActivationFunctionType.Copy
+MULT = mybir.AluOpType.mult
+ADD = mybir.AluOpType.add
+
+P = 128
+PACK = 4
+TILES = E // P
+BANK = 512
+BLOCKS = T // P
+
+
+def tile_attend_headwrite_kernel(tc, emb_words, emb_scales, wv, old, retain, offs, offs2, out):
+    nc = tc.nc
+    with ExitStack() as ctx:
+        keep = ctx.enter_context(tc.tile_pool(name="keep", bufs=1))
+        psum = ctx.enter_context(tc.psum_pool(name="psum", bufs=1))
+
+        old_v = old.rearrange("(p j) t -> p j t", j=TILES)
+        out_v = out.rearrange("(p j) t -> p j t", j=TILES)
+
+        slot_list = keep.tile([P, I // 16], U16, name="slot_list")
+        place_list = keep.tile([P, I // 16], U16, name="place_list")
+        words = keep.tile([P, 2 * U], U8, name="words", tag="words_old01")
+        scales = keep.tile([P, U], U8, name="scales", tag="grouped0", align_bytes=64)
+        w_raw = keep.tile([P, PACK, E], F32, name="w_raw")
+        retain_rows = keep.tile([P, P], F32, name="retain_rows")
+        ident = keep.tile([P, P], F32, name="ident")
+        placed = [keep.tile([P, T], F32, name="placed%d" % j) for j in range(TILES)]
+
+        nc.vector.memset(scales[:].bitcast(I32), 0)
+        nc.gpsimd.memset(retain_rows[:], 0.0)
+        make_identity(nc, ident[:])
+
+        nc.sync.dma_start(slot_list[:], offs)
+        nc.scalar.dma_start(retain_rows[0:BLOCKS, :], retain.rearrange("o (c p) -> (o c) p", p=P))
+        nc.sync.dma_start(words[:].bitcast(I32), emb_words[0].bitcast(I32))
+        for q in range(4):
+            nc.scalar.dma_start(
+                scales[32 * q : 32 * q + 4, :].bitcast(I32), emb_scales[0, 4 * q : 4 * q + 4, :].bitcast(I32)
+            )
+        nc.sync.dma_start(w_raw[:], wv.rearrange("(p t) e -> p t e", t=PACK))
+        nc.sync.dma_start(place_list[:], offs2)
+
+        for j in range(TILES):
+            nc.vector.memset(placed[j][:].bitcast(I32), 0)
+
+        got_words = keep.tile([P, 2 * I], U8, name="got_words", align_bytes=64)
+        got_scales = keep.tile([P, I], U8, name="got_scales", align_bytes=64)
+        nc.vector.tensor_copy(got_words[:].bitcast(U16), words[:].bitcast(U16).indirect(slot_list[:]))
+        nc.vector.tensor_copy(got_scales[:], scales[:].indirect(slot_list[:]))
+
+        turn = psum.tile([P, BANK], F32, name="turn", tag="acc", bufs=3)
+        nc.tensor.transpose(turn[:, 0:P], retain_rows[:], ident[:])
+        old01 = keep.tile([P, 2, T], F32, name="old01", tag="words_old01")
+        nc.sync.dma_start(old01[:, 0, :], old_v[:, 0, :])
+        nc.sync.dma_start(old01[:, 1, :], old_v[:, 1, :])
+        retain_cols = keep.tile([P, BLOCKS], F32, name="retain_cols")
+        nc.scalar.activation(retain_cols[:], turn[:, 0:BLOCKS], COPY)
+        retain_all = keep.tile([P, T], F32, name="retain_all")
+        for b in range(T // BANK):
+            wide = psum.tile([P, BANK], F32, name="wide", tag="acc", bufs=3)
+            for c in range(BANK // P):
+                col = b * (BANK // P) + c
+                nc.tensor.transpose(
+                    wide[:, c * P : (c + 1) * P], retain_cols[:, col : col + 1].to_broadcast([P, P]), ident[:]
+                )
+            nc.scalar.activation(retain_all[:, b * BANK : (b + 1) * BANK], wide[:], COPY)
+
+        w_by_tile = w_raw[:].rearrange("p t (m j) -> p j m t", j=TILES)
+        values = []
+        for j in range(TILES):
+            grouped = keep.tile([P, P, PACK], BF16, name="grouped%d" % j, tag="grouped%d" % j, align_bytes=64)
+            if j < 2:
+                nc.vector.tensor_copy(grouped[:], w_by_tile[:, j])
+            else:
+                nc.scalar.activation(grouped[:], w_by_tile[:, j], COPY)
+            codes = keep.tile([P, P], U32, name="codes%d" % j, align_bytes=64)
+            w_scales = keep.tile([P, P], U8, name="w_scales%d" % j, align_bytes=64)
+            nc.vector.quantize_mx(
+                out=codes[:].bitcast(FP8X4), scales=w_scales[:], in_=grouped[:].rearrange("p m t -> p (m t)")
+            )
+            acc = psum.tile([P, I], F32, name="acc", tag="acc", bufs=3)
+            nc.tensor.matmul_mx(
+                out=acc[:],
+                lhsT=codes[:].bitcast(FP8X4),
+                lhsT_scale=w_scales[:],
+                rhs=got_words[:].bitcast(FP4X4),
+                rhs_scale=got_scales[:],
+                start=True,
+                stop=True,
+            )
+            v = keep.tile([P, I], F32, name="v%d" % j)
+            nc.scalar.activation(v[:], acc[:], COPY)
+            values.append(v)
+
+        old23 = keep.tile([P, 2, T], F32, name="old23", tag="grouped0", align_bytes=64)
+        nc.sync.dma_start(old23[:], old_v[:, 2:4, :])
+
+        kept0 = keep.tile([P, T], F32, name="kept0", tag="grouped3", align_bytes=64)
+        kept1 = keep.tile([P, T], F32, name="kept1")
+        nc.gpsimd.tensor_tensor(kept0[:], old01[:, 0, :], retain_all[:], MULT)
+        nc.gpsimd.tensor_tensor(kept1[:], old01[:, 1, :], retain_all[:], MULT)
+
+        for j in range(TILES):
+            nc.vector.tensor_copy(placed[j][:].indirect(place_list[:]), values[j][:])
+
+        kept2 = keep.tile([P, T], F32, name="kept2")
+        kept3 = []
+        for b in range(T // BANK):
+            back2 = psum.tile([P, BANK], F32, name="back2", tag="wide", bufs=4)
+            back3 = psum.tile([P, BANK], F32, name="back3", tag="wide", bufs=4)
+            for h in range(2):
+                turn = psum.tile([P, BANK], F32, name="turn", tag="acc", bufs=3)
+                turned = keep.tile([P, BANK], F32, name="turned%d" % (2 * b + h))
+                for cc in range(2):
+                    c = 4 * b + 2 * h + cc
+                    for jj in range(2):
+                        at = (2 * cc + jj) * P
+                        nc.tensor.transpose(turn[:, at : at + P], old23[:, jj, c * P : (c + 1) * P], ident[:])
+                for cc in range(2):
+                    c = 4 * b + 2 * h + cc
+                    cols = slice(2 * cc * P, 2 * (cc + 1) * P)
+                    nc.scalar.activation(turned[:, cols], turn[:, cols], COPY, scale=retain_cols[:, c : c + 1])
+                for cc in range(2):
+                    at = (2 * h + cc) * P
+                    for jj, back in enumerate((back2, back3)):
+                        src = (2 * cc + jj) * P
+                        nc.tensor.transpose(back[:, at : at + P], turned[:, src : src + P], ident[:])
+            nc.scalar.activation(kept2[:, b * BANK : (b + 1) * BANK], back2[:], COPY)
+            kept3.append(back3)
+
+        for j, kept in enumerate((kept0, kept1, kept2)):
+            nc.gpsimd.tensor_tensor(kept[:], kept[:], placed[j][:], ADD)
+            nc.sync.dma_start(out_v[:, j, :], kept[:])
+
+        for b in range(T // BANK):
+            last = keep.tile([P, BANK], F32, name="last%d" % b)
+            cols = slice(b * BANK, (b + 1) * BANK)
+            nc.vector.tensor_tensor(last[:], kept3[b][:], placed[3][:, cols], ADD)
+            nc.sync.dma_start(out_v[:, 3, cols], last[:])

@@ -15,7 +15,6 @@ U8 = mybir.dt.uint8
 FP8X4 = mybir.dt.float8_e4m3fn_x4
 FP4X4 = mybir.dt.float4_e2m1fn_x4
 COPY = mybir.ActivationFunctionType.Copy
-MULT = mybir.AluOpType.mult
 ADD = mybir.AluOpType.add
 
 P = 128
@@ -23,6 +22,7 @@ PACK = 4
 TILES = E // P
 BANK = 512
 BLOCKS = T // P
+HALF = I // 2
 
 
 def tile_attend_headwrite_kernel(tc, emb_words, emb_scales, wv, old, retain, offs, offs2, out):
@@ -36,121 +36,117 @@ def tile_attend_headwrite_kernel(tc, emb_words, emb_scales, wv, old, retain, off
 
         slot_list = keep.tile([P, I // 16], U16, name="slot_list")
         place_list = keep.tile([P, I // 16], U16, name="place_list")
-        words = keep.tile([P, 2 * U], U8, name="words", tag="words_old01")
+        words = keep.tile([P, 2 * U], U8, name="words", tag="words_old")
         scales = keep.tile([P, U], U8, name="scales", tag="grouped0", align_bytes=64)
-        w_raw = keep.tile([P, PACK, E], F32, name="w_raw")
+        zeros = keep.tile([P, P], F32, name="zeros", tag="zeros_w")
         retain_rows = keep.tile([P, P], F32, name="retain_rows")
         ident = keep.tile([P, P], F32, name="ident")
-        placed = [keep.tile([P, T], F32, name="placed%d" % j) for j in range(TILES)]
+        placed = [keep.tile([P, T], F32, name="placed%d" % i) for i in range(2)]
 
         nc.vector.memset(scales[:].bitcast(I32), 0)
-        nc.gpsimd.memset(retain_rows[:], 0.0)
+        nc.vector.memset(zeros[:], 0.0)
+        nc.vector.tensor_copy(retain_rows[:], zeros[:])
         make_identity(nc, ident[:])
 
         nc.sync.dma_start(slot_list[:], offs)
-        nc.scalar.dma_start(retain_rows[0:BLOCKS, :], retain.rearrange("o (c p) -> (o c) p", p=P))
         nc.sync.dma_start(words[:].bitcast(I32), emb_words[0].bitcast(I32))
-        for q in range(4):
-            nc.scalar.dma_start(
-                scales[32 * q : 32 * q + 4, :].bitcast(I32), emb_scales[0, 4 * q : 4 * q + 4, :].bitcast(I32)
-            )
+        for r in range(4):
+            nc.sync.dma_start(scales[r:P:32, :].bitcast(I32), emb_scales[0, r:16:4, :].bitcast(I32))
+        nc.scalar.dma_start(retain_rows[0:BLOCKS, :], retain.rearrange("o (c p) -> (o c) p", p=P))
+        w_raw = keep.tile([P, PACK, E], F32, name="w_raw", tag="zeros_w")
         nc.sync.dma_start(w_raw[:], wv.rearrange("(p t) e -> p t e", t=PACK))
         nc.sync.dma_start(place_list[:], offs2)
 
-        for j in range(TILES):
-            nc.vector.memset(placed[j][:].bitcast(I32), 0)
+        for i in range(2):
+            nc.vector.memset(placed[i][:].bitcast(I32), 0)
 
         got_words = keep.tile([P, 2 * I], U8, name="got_words", align_bytes=64)
         got_scales = keep.tile([P, I], U8, name="got_scales", align_bytes=64)
         nc.vector.tensor_copy(got_words[:].bitcast(U16), words[:].bitcast(U16).indirect(slot_list[:]))
         nc.vector.tensor_copy(got_scales[:], scales[:].indirect(slot_list[:]))
 
-        turn = psum.tile([P, BANK], F32, name="turn", tag="acc", bufs=3)
+        turn = psum.tile([P, BANK], F32, name="turn", tag="stream", bufs=2)
         nc.tensor.transpose(turn[:, 0:P], retain_rows[:], ident[:])
-        old01 = keep.tile([P, 2, T], F32, name="old01", tag="words_old01")
-        nc.sync.dma_start(old01[:, 0, :], old_v[:, 0, :])
-        nc.sync.dma_start(old01[:, 1, :], old_v[:, 1, :])
         retain_cols = keep.tile([P, BLOCKS], F32, name="retain_cols")
         nc.scalar.activation(retain_cols[:], turn[:, 0:BLOCKS], COPY)
-        retain_all = keep.tile([P, T], F32, name="retain_all")
-        for b in range(T // BANK):
-            wide = psum.tile([P, BANK], F32, name="wide", tag="acc", bufs=3)
-            for c in range(BANK // P):
-                col = b * (BANK // P) + c
-                nc.tensor.transpose(
-                    wide[:, c * P : (c + 1) * P], retain_cols[:, col : col + 1].to_broadcast([P, P]), ident[:]
-                )
-            nc.scalar.activation(retain_all[:, b * BANK : (b + 1) * BANK], wide[:], COPY)
 
-        w_by_tile = w_raw[:].rearrange("p t (m j) -> p j m t", j=TILES)
+        old_pair = [keep.tile([P, 2, T], F32, name="old01", tag="words_old")]
+        for jj in range(2):
+            nc.sync.dma_start(old_pair[0][:, jj, :], old_v[:, jj, :])
+
+        w_by_col = w_raw[:].rearrange("p t (m j) -> p m j t", j=TILES)
         values = []
-        for j in range(TILES):
-            grouped = keep.tile([P, P, PACK], BF16, name="grouped%d" % j, tag="grouped%d" % j, align_bytes=64)
-            if j < 2:
-                nc.vector.tensor_copy(grouped[:], w_by_tile[:, j])
+        for pair in range(2):
+            grouped = keep.tile([P, 2, P, PACK], BF16, name="grouped%d" % pair, tag="grouped%d" % pair, align_bytes=64)
+            dealt = grouped[:].rearrange("p j m t -> p m j t")
+            if pair == 0:
+                nc.vector.tensor_copy(dealt, w_by_col[:, :, 0:2, :])
             else:
-                nc.scalar.activation(grouped[:], w_by_tile[:, j], COPY)
-            codes = keep.tile([P, P], U32, name="codes%d" % j, align_bytes=64)
-            w_scales = keep.tile([P, P], U8, name="w_scales%d" % j, align_bytes=64)
-            nc.vector.quantize_mx(
-                out=codes[:].bitcast(FP8X4), scales=w_scales[:], in_=grouped[:].rearrange("p m t -> p (m t)")
-            )
-            acc = psum.tile([P, I], F32, name="acc", tag="acc", bufs=3)
-            nc.tensor.matmul_mx(
-                out=acc[:],
-                lhsT=codes[:].bitcast(FP8X4),
-                lhsT_scale=w_scales[:],
-                rhs=got_words[:].bitcast(FP4X4),
-                rhs_scale=got_scales[:],
-                start=True,
-                stop=True,
-            )
-            v = keep.tile([P, I], F32, name="v%d" % j)
-            nc.scalar.activation(v[:], acc[:], COPY)
-            values.append(v)
+                nc.scalar.activation(dealt, w_by_col[:, :, 2:4, :], COPY)
+            for jj in range(2):
+                j = 2 * pair + jj
+                codes = keep.tile([P, P], U32, name="codes%d" % j, align_bytes=64)
+                w_scales = keep.tile([P, P], U8, name="w_scales%d" % j, align_bytes=64)
+                nc.vector.quantize_mx(
+                    out=codes[:].bitcast(FP8X4),
+                    scales=w_scales[:],
+                    in_=grouped[:, jj].rearrange("p m t -> p (m t)"),
+                )
+                parts = 2 if j == 0 else 1
+                width = I // parts
+                pieces = []
+                for h in range(parts):
+                    acc = psum.tile([P, BANK], F32, name="acc", tag="stream" if j == 1 or h == 1 else "late", bufs=2)
+                    nc.tensor.matmul_mx(
+                        out=acc[:, 0:width],
+                        lhsT=codes[:].bitcast(FP8X4),
+                        lhsT_scale=w_scales[:],
+                        rhs=got_words[:, 2 * h * width : 2 * (h + 1) * width].bitcast(FP4X4),
+                        rhs_scale=got_scales[:, h * width : (h + 1) * width],
+                        start=True,
+                        stop=True,
+                    )
+                    v = keep.tile([P, width], F32, name="v%d_%d" % (j, h))
+                    nc.scalar.activation(v[:], acc[:, 0:width], COPY)
+                    pieces.append((v, place_list[:, h * width // 16 : (h + 1) * width // 16]))
+                values.append(pieces)
 
-        old23 = keep.tile([P, 2, T], F32, name="old23", tag="grouped0", align_bytes=64)
-        nc.sync.dma_start(old23[:], old_v[:, 2:4, :])
+        old_pair.append(keep.tile([P, 2, T], F32, name="old23", tag="grouped0", align_bytes=64))
+        nc.sync.dma_start(old_pair[1][:], old_v[:, 2:4, :])
 
-        kept0 = keep.tile([P, T], F32, name="kept0", tag="grouped3", align_bytes=64)
-        kept1 = keep.tile([P, T], F32, name="kept1")
-        nc.gpsimd.tensor_tensor(kept0[:], old01[:, 0, :], retain_all[:], MULT)
-        nc.gpsimd.tensor_tensor(kept1[:], old01[:, 1, :], retain_all[:], MULT)
-
-        for j in range(TILES):
-            nc.vector.tensor_copy(placed[j][:].indirect(place_list[:]), values[j][:])
-
-        kept2 = keep.tile([P, T], F32, name="kept2")
-        kept3 = []
-        for b in range(T // BANK):
-            back2 = psum.tile([P, BANK], F32, name="back2", tag="wide", bufs=4)
-            back3 = psum.tile([P, BANK], F32, name="back3", tag="wide", bufs=4)
-            for h in range(2):
-                turn = psum.tile([P, BANK], F32, name="turn", tag="acc", bufs=3)
-                turned = keep.tile([P, BANK], F32, name="turned%d" % (2 * b + h))
-                for cc in range(2):
-                    c = 4 * b + 2 * h + cc
-                    for jj in range(2):
-                        at = (2 * cc + jj) * P
-                        nc.tensor.transpose(turn[:, at : at + P], old23[:, jj, c * P : (c + 1) * P], ident[:])
-                for cc in range(2):
-                    c = 4 * b + 2 * h + cc
-                    cols = slice(2 * cc * P, 2 * (cc + 1) * P)
-                    nc.scalar.activation(turned[:, cols], turn[:, cols], COPY, scale=retain_cols[:, c : c + 1])
-                for cc in range(2):
-                    at = (2 * h + cc) * P
-                    for jj, back in enumerate((back2, back3)):
-                        src = (2 * cc + jj) * P
-                        nc.tensor.transpose(back[:, at : at + P], turned[:, src : src + P], ident[:])
-            nc.scalar.activation(kept2[:, b * BANK : (b + 1) * BANK], back2[:], COPY)
-            kept3.append(back3)
-
-        for j, kept in enumerate((kept0, kept1, kept2)):
-            nc.gpsimd.tensor_tensor(kept[:], kept[:], placed[j][:], ADD)
-            nc.sync.dma_start(out_v[:, j, :], kept[:])
-
-        for b in range(T // BANK):
-            last = keep.tile([P, BANK], F32, name="last%d" % b)
-            cols = slice(b * BANK, (b + 1) * BANK)
-            nc.vector.tensor_tensor(last[:], kept3[b][:], placed[3][:, cols], ADD)
-            nc.sync.dma_start(out_v[:, 3, cols], last[:])
+        for pair in range(2):
+            for jj in range(2):
+                for v, places in values[2 * pair + jj]:
+                    nc.vector.tensor_copy(placed[jj][:].indirect(places), v[:])
+            kept = [[], []]
+            for b in range(T // BANK):
+                for jj in range(2):
+                    kept[jj].append(psum.tile([P, BANK], F32, name="kept", tag="kept", bufs=4))
+                for h in range(2):
+                    turn = psum.tile([P, BANK], F32, name="turn", tag="stream", bufs=2)
+                    turned = keep.tile([P, BANK], F32, name="turned%d" % (4 * pair + 2 * b + h))
+                    for cc in range(2):
+                        c = 4 * b + 2 * h + cc
+                        for jj in range(2):
+                            at = (2 * cc + jj) * P
+                            nc.tensor.transpose(
+                                turn[:, at : at + P], old_pair[pair][:, jj, c * P : (c + 1) * P], ident[:]
+                            )
+                    for cc in range(2):
+                        c = 4 * b + 2 * h + cc
+                        cols = slice(2 * cc * P, 2 * (cc + 1) * P)
+                        nc.scalar.activation(turned[:, cols], turn[:, cols], COPY, scale=retain_cols[:, c : c + 1])
+                    for cc in range(2):
+                        at = (2 * h + cc) * P
+                        for jj in range(2):
+                            src = (2 * cc + jj) * P
+                            nc.tensor.transpose(kept[jj][b][:, at : at + P], turned[:, src : src + P], ident[:])
+            for jj in range(2):
+                j = 2 * pair + jj
+                for b in range(T // BANK):
+                    cols = slice(b * BANK, (b + 1) * BANK)
+                    res = keep.tile([P, BANK], F32, name="res%d_%d" % (j, b))
+                    nc.vector.tensor_tensor(res[:], kept[jj][b][:], placed[jj][:, cols], ADD)
+                    nc.sync.dma_start(out_v[:, j, cols], res[:])
+                    if pair == 0:
+                        nc.gpsimd.memset(placed[jj][:, cols].bitcast(I32), 0)

@@ -16,6 +16,7 @@ FP8X4 = mybir.dt.float8_e4m3fn_x4
 FP4X4 = mybir.dt.float4_e2m1fn_x4
 COPY = mybir.ActivationFunctionType.Copy
 ADD = mybir.AluOpType.add
+MULT = mybir.AluOpType.mult
 
 P = 128
 PACK = 4
@@ -36,23 +37,24 @@ def tile_attend_headwrite_kernel(tc, emb_words, emb_scales, wv, old, retain, off
 
         slot_list = keep.tile([P, I // 16], U16, name="slot_list")
         place_list = keep.tile([P, I // 16], U16, name="place_list")
-        words = keep.tile([P, 2 * U], U8, name="words", tag="words_old")
+        words = keep.tile([P, 2 * U], U8, name="words", tag="words_old1")
         scales = keep.tile([P, U], U8, name="scales", tag="grouped0", align_bytes=64)
         zeros = keep.tile([P, P], F32, name="zeros", tag="zeros_w")
-        retain_rows = keep.tile([P, P], F32, name="retain_rows")
+        retain_rows = keep.tile([P, P], F32, name="retain_rows", tag="rows_old")
         ident = keep.tile([P, P], F32, name="ident")
         placed = [keep.tile([P, T], F32, name="placed%d" % i) for i in range(2)]
 
-        nc.vector.memset(scales[:].bitcast(I32), 0)
         nc.vector.memset(zeros[:], 0.0)
-        nc.vector.tensor_copy(retain_rows[:], zeros[:])
-        make_identity(nc, ident[:])
+        nc.vector.memset(scales[:].bitcast(I32), 0)
+        nc.vector.tensor_copy(ident[:], zeros[:])
+        nc.gpsimd.memset(retain_rows[:], 0.0)
+        nc.gpsimd.dma_start(retain_rows[0:BLOCKS, :], retain.rearrange("o (c p) -> (o c) p", p=P))
+        make_identity(nc, ident[:], nomemset=True)
 
         nc.sync.dma_start(slot_list[:], offs)
         nc.sync.dma_start(words[:].bitcast(I32), emb_words[0].bitcast(I32))
         for r in range(4):
             nc.sync.dma_start(scales[r:P:32, :].bitcast(I32), emb_scales[0, r:16:4, :].bitcast(I32))
-        nc.scalar.dma_start(retain_rows[0:BLOCKS, :], retain.rearrange("o (c p) -> (o c) p", p=P))
         w_raw = keep.tile([P, PACK, E], F32, name="w_raw", tag="zeros_w")
         nc.sync.dma_start(w_raw[:], wv.rearrange("(p t) e -> p t e", t=PACK))
         nc.sync.dma_start(place_list[:], offs2)
@@ -69,10 +71,20 @@ def tile_attend_headwrite_kernel(tc, emb_words, emb_scales, wv, old, retain, off
         nc.tensor.transpose(turn[:, 0:P], retain_rows[:], ident[:])
         retain_cols = keep.tile([P, BLOCKS], F32, name="retain_cols")
         nc.scalar.activation(retain_cols[:], turn[:, 0:BLOCKS], COPY)
+        retain_all = keep.tile([P, T], F32, name="retain_all")
+        for b in range(T // BANK):
+            spread = psum.tile([P, BANK], F32, name="spread", tag="back", bufs=4)
+            for c in range(BANK // P):
+                col = b * (BANK // P) + c
+                nc.tensor.transpose(
+                    spread[:, c * P : (c + 1) * P], retain_cols[:, col : col + 1].to_broadcast([P, P]), ident[:]
+                )
+            nc.scalar.activation(retain_all[:, b * BANK : (b + 1) * BANK], spread[:], COPY)
 
-        old_pair = [keep.tile([P, 2, T], F32, name="old01", tag="words_old")]
-        for jj in range(2):
-            nc.sync.dma_start(old_pair[0][:, jj, :], old_v[:, jj, :])
+        old0 = keep.tile([P, T], F32, name="old0", tag="rows_old")
+        nc.sync.dma_start(old0[:], old_v[:, 0, :])
+        old1 = keep.tile([P, T], F32, name="old1", tag="words_old1")
+        nc.sync.dma_start(old1[:], old_v[:, 1, :])
 
         w_by_col = w_raw[:].rearrange("p t (m j) -> p m j t", j=TILES)
         values = []
@@ -111,42 +123,50 @@ def tile_attend_headwrite_kernel(tc, emb_words, emb_scales, wv, old, retain, off
                     pieces.append((v, place_list[:, h * width // 16 : (h + 1) * width // 16]))
                 values.append(pieces)
 
-        old_pair.append(keep.tile([P, 2, T], F32, name="old23", tag="grouped0", align_bytes=64))
-        nc.sync.dma_start(old_pair[1][:], old_v[:, 2:4, :])
+        old23 = keep.tile([P, 2, T], F32, name="old23", tag="zeros_w")
+        nc.sync.dma_start(old23[:], old_v[:, 2:4, :])
+        placed.append(keep.tile([P, T], F32, name="placed2", tag="grouped0", align_bytes=64))
+        nc.vector.memset(placed[2][:].bitcast(I32), 0)
 
-        for pair in range(2):
-            for jj in range(2):
-                for v, places in values[2 * pair + jj]:
-                    nc.vector.tensor_copy(placed[jj][:].indirect(places), v[:])
-            kept = [[], []]
-            for b in range(T // BANK):
-                for jj in range(2):
-                    kept[jj].append(psum.tile([P, BANK], F32, name="kept", tag="kept", bufs=4))
-                for h in range(2):
-                    turn = psum.tile([P, BANK], F32, name="turn", tag="stream", bufs=2)
-                    turned = keep.tile([P, BANK], F32, name="turned%d" % (4 * pair + 2 * b + h))
-                    for cc in range(2):
-                        c = 4 * b + 2 * h + cc
-                        for jj in range(2):
-                            at = (2 * cc + jj) * P
-                            nc.tensor.transpose(
-                                turn[:, at : at + P], old_pair[pair][:, jj, c * P : (c + 1) * P], ident[:]
-                            )
-                    for cc in range(2):
-                        c = 4 * b + 2 * h + cc
-                        cols = slice(2 * cc * P, 2 * (cc + 1) * P)
-                        nc.scalar.activation(turned[:, cols], turn[:, cols], COPY, scale=retain_cols[:, c : c + 1])
-                    for cc in range(2):
-                        at = (2 * h + cc) * P
-                        for jj in range(2):
-                            src = (2 * cc + jj) * P
-                            nc.tensor.transpose(kept[jj][b][:, at : at + P], turned[:, src : src + P], ident[:])
-            for jj in range(2):
-                j = 2 * pair + jj
-                for b in range(T // BANK):
-                    cols = slice(b * BANK, (b + 1) * BANK)
-                    res = keep.tile([P, BANK], F32, name="res%d_%d" % (j, b))
-                    nc.vector.tensor_tensor(res[:], kept[jj][b][:], placed[jj][:, cols], ADD)
-                    nc.sync.dma_start(out_v[:, j, cols], res[:])
-                    if pair == 0:
-                        nc.gpsimd.memset(placed[jj][:, cols].bitcast(I32), 0)
+        kept0 = keep.tile([P, T], F32, name="kept0", tag="grouped1", align_bytes=64)
+        nc.gpsimd.tensor_tensor(kept0[:], old0[:], retain_all[:], MULT)
+        nc.gpsimd.tensor_tensor(old1[:], old1[:], retain_all[:], MULT)
+
+        kept2 = keep.tile([P, T], F32, name="kept2")
+        kept3 = []
+        for b in range(T // BANK):
+            back2 = psum.tile([P, BANK], F32, name="back2", tag="back", bufs=4)
+            back3 = psum.tile([P, BANK], F32, name="back3", tag="back", bufs=4)
+            for h in range(2):
+                turn = psum.tile([P, BANK], F32, name="turn", tag="stream", bufs=2)
+                turned = keep.tile([P, BANK], F32, name="turned%d" % (2 * b + h))
+                for cc in range(2):
+                    c = 4 * b + 2 * h + cc
+                    for jj in range(2):
+                        at = (2 * cc + jj) * P
+                        nc.tensor.transpose(turn[:, at : at + P], old23[:, jj, c * P : (c + 1) * P], ident[:])
+                for cc in range(2):
+                    c = 4 * b + 2 * h + cc
+                    cols = slice(2 * cc * P, 2 * (cc + 1) * P)
+                    nc.scalar.activation(turned[:, cols], turn[:, cols], COPY, scale=retain_cols[:, c : c + 1])
+                for cc in range(2):
+                    at = (2 * h + cc) * P
+                    for jj, back in enumerate((back2, back3)):
+                        src = (2 * cc + jj) * P
+                        nc.tensor.transpose(back[:, at : at + P], turned[:, src : src + P], ident[:])
+            nc.scalar.activation(kept2[:, b * BANK : (b + 1) * BANK], back2[:], COPY)
+            kept3.append(back3)
+
+        for j, kept in enumerate((kept0, old1, kept2)):
+            for v, places in values[j]:
+                nc.vector.tensor_copy(placed[j][:].indirect(places), v[:])
+            nc.gpsimd.tensor_tensor(kept[:], kept[:], placed[j][:], ADD)
+            nc.sync.dma_start(out_v[:, j, :], kept[:])
+
+        for v, places in values[3]:
+            nc.vector.tensor_copy(placed[0][:].indirect(places), v[:])
+        last = keep.tile([P, T], F32, name="last", tag="grouped0", align_bytes=64)
+        for b in range(T // BANK):
+            cols = slice(b * BANK, (b + 1) * BANK)
+            nc.vector.tensor_tensor(last[:, cols], kept3[b][:], placed[0][:, cols], ADD)
+            nc.sync.dma_start(out_v[:, 3, cols], last[:, cols])

@@ -31,49 +31,93 @@ def tile_attend_headwrite_kernel(tc, emb_words, emb_scales, wv, old, retain, off
     with ExitStack() as ctx:
         keep = ctx.enter_context(tc.tile_pool(name="keep", bufs=1))
         psum = ctx.enter_context(tc.psum_pool(name="psum", bufs=1))
+        bank = [psum.tile([P, BANK], F32, name="bank%d" % b) for b in range(8)]
 
         old_v = old.rearrange("(p j) t -> p j t", j=TILES)
         out_v = out.rearrange("(p j) t -> p j t", j=TILES)
 
         slot_list = keep.tile([P, I // 16], U16, name="slot_list")
         place_list = keep.tile([P, I // 16], U16, name="place_list")
-        words = keep.tile([P, 2 * U], U8, name="words", tag="words_old1")
-        scales = keep.tile([P, U], U8, name="scales", tag="grouped0", align_bytes=64)
-        zeros = keep.tile([P, P], F32, name="zeros", tag="zeros_w")
-        retain_rows = keep.tile([P, P], F32, name="retain_rows", tag="rows_old")
+        zeros = keep.tile([P, P], F32, name="zeros", tag="zeros_words")
+        scales = keep.tile([P, U], U8, name="scales", tag="scales_old0")
+        w_raw = keep.tile([P, PACK, E], F32, name="w_raw", tag="w_old0")
+        retain_rows = keep.tile([P, P], F32, name="retain_rows")
         ident = keep.tile([P, P], F32, name="ident")
         placed = [keep.tile([P, T], F32, name="placed%d" % i) for i in range(2)]
 
-        nc.vector.memset(zeros[:], 0.0)
-        nc.vector.memset(scales[:].bitcast(I32), 0)
-        nc.vector.tensor_copy(ident[:], zeros[:])
-        nc.gpsimd.memset(retain_rows[:], 0.0)
-        nc.gpsimd.dma_start(retain_rows[0:BLOCKS, :], retain.rearrange("o (c p) -> (o c) p", p=P))
-        make_identity(nc, ident[:], nomemset=True)
-
+        wv_v = wv.rearrange("(p t) e -> p t e", t=PACK)
         nc.sync.dma_start(slot_list[:], offs)
-        nc.sync.dma_start(words[:].bitcast(I32), emb_words[0].bitcast(I32))
-        for r in range(4):
-            nc.sync.dma_start(scales[r:P:32, :].bitcast(I32), emb_scales[0, r:16:4, :].bitcast(I32))
-        w_raw = keep.tile([P, PACK, E], F32, name="w_raw", tag="zeros_w")
-        nc.sync.dma_start(w_raw[:], wv.rearrange("(p t) e -> p t e", t=PACK))
+        nc.sync.dma_start(w_raw[:, 0:2, :], wv_v[:, 0:2, :])
         nc.sync.dma_start(place_list[:], offs2)
 
-        for i in range(2):
-            nc.vector.memset(placed[i][:].bitcast(I32), 0)
+        nc.vector.memset(w_raw[:, 3, 0:P], 0.0)
+        nc.vector.memset(zeros[:], 0.0)
+        nc.vector.memset(scales[:].bitcast(I32), 0)
+        for r in range(4):
+            nc.sync.dma_start(scales[r:P:32, :].bitcast(I32), emb_scales[0, r:16:4, :].bitcast(I32))
+        nc.vector.tensor_copy(retain_rows[:], w_raw[:, 3, 0:P])
+        nc.scalar.activation(ident[:], zeros[:], COPY)
+        make_identity(nc, ident[:], nomemset=True)
+        nc.sync.dma_start(w_raw[:, 2:4, :], wv_v[:, 2:4, :])
+        words = keep.tile([P, 2 * U], U8, name="words", tag="zeros_words")
+        nc.sync.dma_start(words[:].bitcast(I32), emb_words[0].bitcast(I32))
+        nc.sync.dma_start(retain_rows[0:BLOCKS, :], retain.rearrange("o (c p) -> (o c) p", p=P))
+        for window in placed:
+            nc.vector.memset(window[:].bitcast(I32), 0)
 
         got_words = keep.tile([P, 2 * I], U8, name="got_words", align_bytes=64)
         got_scales = keep.tile([P, I], U8, name="got_scales", align_bytes=64)
-        nc.vector.tensor_copy(got_words[:].bitcast(U16), words[:].bitcast(U16).indirect(slot_list[:]))
         nc.vector.tensor_copy(got_scales[:], scales[:].indirect(slot_list[:]))
 
-        turn = psum.tile([P, BANK], F32, name="turn", tag="stream", bufs=2)
-        nc.tensor.transpose(turn[:, 0:P], retain_rows[:], ident[:])
+        w_by_col = w_raw[:].rearrange("p t (m j) -> p m j t", j=TILES)
+        grouped = [
+            keep.tile([P, 2, P, PACK], BF16, name="grouped%d" % g, tag="grouped%d" % g, align_bytes=64)
+            for g in range(2)
+        ]
+        nc.vector.tensor_copy(grouped[0][:].rearrange("p j m t -> p m j t"), w_by_col[:, :, 0:2, :])
+        nc.scalar.activation(grouped[1][:].rearrange("p j m t -> p m j t"), w_by_col[:, :, 2:4, :], COPY)
+
+        codes = keep.tile([P, E], U32, name="codes", align_bytes=64)
+        w_scales = keep.tile([P, E], U8, name="w_scales", align_bytes=64)
+
+        def quantise(j0, j1):
+            nc.vector.quantize_mx(
+                out=codes[:, j0 * P : j1 * P].bitcast(FP8X4),
+                scales=w_scales[:, j0 * P : j1 * P],
+                in_=grouped[j0 // 2][:, j0 % 2 : j0 % 2 + j1 - j0].rearrange("p j m t -> p (j m t)"),
+            )
+
+        def project(j, i0, i1, acc):
+            nc.tensor.matmul_mx(
+                out=acc[:, 0 : i1 - i0],
+                lhsT=codes[:, j * P : (j + 1) * P].bitcast(FP8X4),
+                lhsT_scale=w_scales[:, j * P : (j + 1) * P],
+                rhs=got_words[:, 2 * i0 : 2 * i1].bitcast(FP4X4),
+                rhs_scale=got_scales[:, i0:i1],
+                start=True,
+                stop=True,
+            )
+            v = keep.tile([P, i1 - i0], F32, name="v%d_%d" % (j, i0))
+            nc.scalar.activation(v[:], acc[:, 0 : i1 - i0], COPY)
+            return v, place_list[:, i0 // 16 : i1 // 16]
+
+        quantise(0, 2)
+        for h in range(2):
+            nc.vector.tensor_copy(
+                got_words[:, 2 * h * HALF : 2 * (h + 1) * HALF].bitcast(U16),
+                words[:].bitcast(U16).indirect(slot_list[:, h * HALF // 16 : (h + 1) * HALF // 16]),
+            )
+        quantise(2, 4)
+
+        nc.tensor.transpose(bank[0][:, 0:P], retain_rows[:], ident[:])
         retain_cols = keep.tile([P, BLOCKS], F32, name="retain_cols")
-        nc.scalar.activation(retain_cols[:], turn[:, 0:BLOCKS], COPY)
+        nc.scalar.activation(retain_cols[:], bank[0][:, 0:BLOCKS], COPY)
+
+        values = [[project(0, 0, HALF, bank[1]), project(0, HALF, I, bank[2])], [project(1, 0, I, bank[3])]]
+
         retain_all = keep.tile([P, T], F32, name="retain_all")
         for b in range(T // BANK):
-            spread = psum.tile([P, BANK], F32, name="spread", tag="back", bufs=4)
+            spread = bank[1 + b]
             for c in range(BANK // P):
                 col = b * (BANK // P) + c
                 nc.tensor.transpose(
@@ -81,92 +125,54 @@ def tile_attend_headwrite_kernel(tc, emb_words, emb_scales, wv, old, retain, off
                 )
             nc.scalar.activation(retain_all[:, b * BANK : (b + 1) * BANK], spread[:], COPY)
 
-        old0 = keep.tile([P, T], F32, name="old0", tag="rows_old")
+        values.append([project(2, 0, I, bank[0])])
+        values.append([project(3, 0, I, bank[4])])
+
+        old0 = keep.tile([P, T], F32, name="old0", tag="scales_old0")
         nc.sync.dma_start(old0[:], old_v[:, 0, :])
-        old1 = keep.tile([P, T], F32, name="old1", tag="words_old1")
-        nc.sync.dma_start(old1[:], old_v[:, 1, :])
+        old_rest = keep.tile([P, (TILES - 1) * T], F32, name="old_rest", tag="w_old0")
+        for j in range(1, TILES):
+            nc.sync.dma_start(old_rest[:, (j - 1) * T : j * T], old_v[:, j, :])
 
-        w_by_col = w_raw[:].rearrange("p t (m j) -> p m j t", j=TILES)
-        values = []
-        for pair in range(2):
-            grouped = keep.tile([P, 2, P, PACK], BF16, name="grouped%d" % pair, tag="grouped%d" % pair, align_bytes=64)
-            dealt = grouped[:].rearrange("p j m t -> p m j t")
-            if pair == 0:
-                nc.vector.tensor_copy(dealt, w_by_col[:, :, 0:2, :])
-            else:
-                nc.scalar.activation(dealt, w_by_col[:, :, 2:4, :], COPY)
-            for jj in range(2):
-                j = 2 * pair + jj
-                codes = keep.tile([P, P], U32, name="codes%d" % j, align_bytes=64)
-                w_scales = keep.tile([P, P], U8, name="w_scales%d" % j, align_bytes=64)
-                nc.vector.quantize_mx(
-                    out=codes[:].bitcast(FP8X4),
-                    scales=w_scales[:],
-                    in_=grouped[:, jj].rearrange("p m t -> p (m t)"),
-                )
-                parts = 2 if j == 0 else 1
-                width = I // parts
-                pieces = []
-                for h in range(parts):
-                    acc = psum.tile([P, BANK], F32, name="acc", tag="stream" if j == 1 or h == 1 else "late", bufs=2)
-                    nc.tensor.matmul_mx(
-                        out=acc[:, 0:width],
-                        lhsT=codes[:].bitcast(FP8X4),
-                        lhsT_scale=w_scales[:],
-                        rhs=got_words[:, 2 * h * width : 2 * (h + 1) * width].bitcast(FP4X4),
-                        rhs_scale=got_scales[:, h * width : (h + 1) * width],
-                        start=True,
-                        stop=True,
-                    )
-                    v = keep.tile([P, width], F32, name="v%d_%d" % (j, h))
-                    nc.scalar.activation(v[:], acc[:, 0:width], COPY)
-                    pieces.append((v, place_list[:, h * width // 16 : (h + 1) * width // 16]))
-                values.append(pieces)
+        placed.append(keep.tile([P, T], F32, name="placed2", tag="grouped1", align_bytes=64))
+        nc.gpsimd.memset(placed[2][:].bitcast(I32), 0)
+        nc.gpsimd.tensor_tensor(old0[:], old0[:], retain_all[:], MULT)
 
-        old23 = keep.tile([P, 2, T], F32, name="old23", tag="zeros_w")
-        nc.sync.dma_start(old23[:], old_v[:, 2:4, :])
-        placed.append(keep.tile([P, T], F32, name="placed2", tag="grouped0", align_bytes=64))
-        nc.vector.memset(placed[2][:].bitcast(I32), 0)
-
-        kept0 = keep.tile([P, T], F32, name="kept0", tag="grouped1", align_bytes=64)
-        nc.gpsimd.tensor_tensor(kept0[:], old0[:], retain_all[:], MULT)
-        nc.gpsimd.tensor_tensor(old1[:], old1[:], retain_all[:], MULT)
-
-        kept2 = keep.tile([P, T], F32, name="kept2")
-        kept3 = []
-        for b in range(T // BANK):
-            back2 = psum.tile([P, BANK], F32, name="back2", tag="back", bufs=4)
-            back3 = psum.tile([P, BANK], F32, name="back3", tag="back", bufs=4)
-            for h in range(2):
-                turn = psum.tile([P, BANK], F32, name="turn", tag="stream", bufs=2)
-                turned = keep.tile([P, BANK], F32, name="turned%d" % (2 * b + h))
-                for cc in range(2):
-                    c = 4 * b + 2 * h + cc
-                    for jj in range(2):
-                        at = (2 * cc + jj) * P
-                        nc.tensor.transpose(turn[:, at : at + P], old23[:, jj, c * P : (c + 1) * P], ident[:])
-                for cc in range(2):
-                    c = 4 * b + 2 * h + cc
-                    cols = slice(2 * cc * P, 2 * (cc + 1) * P)
+        kept = [old0]
+        for j in range(1, TILES):
+            if j < TILES - 1:
+                kept.append(keep.tile([P, T], F32, name="kept%d" % j))
+            for b in range(T // BANK):
+                step = 2 * (j - 1) + b
+                turn = bank[step % 3]
+                back = bank[6 + b] if j == TILES - 1 else bank[3 + step % 3]
+                turned = keep.tile([P, BANK], F32, name="turned%d" % step)
+                for cc in range(4):
+                    at = (j - 1) * T + b * BANK + cc * P
+                    nc.tensor.transpose(turn[:, cc * P : (cc + 1) * P], old_rest[:, at : at + P], ident[:])
+                for cc in range(4):
+                    c = 4 * b + cc
+                    cols = slice(cc * P, (cc + 1) * P)
                     nc.scalar.activation(turned[:, cols], turn[:, cols], COPY, scale=retain_cols[:, c : c + 1])
-                for cc in range(2):
-                    at = (2 * h + cc) * P
-                    for jj, back in enumerate((back2, back3)):
-                        src = (2 * cc + jj) * P
-                        nc.tensor.transpose(back[:, at : at + P], turned[:, src : src + P], ident[:])
-            nc.scalar.activation(kept2[:, b * BANK : (b + 1) * BANK], back2[:], COPY)
-            kept3.append(back3)
+                for cc in range(4):
+                    cols = slice(cc * P, (cc + 1) * P)
+                    nc.tensor.transpose(back[:, cols], turned[:, cols], ident[:])
+                if j < TILES - 1:
+                    nc.scalar.activation(kept[j][:, b * BANK : (b + 1) * BANK], back[:], COPY)
 
-        for j, kept in enumerate((kept0, old1, kept2)):
+        for j in range(TILES - 1):
             for v, places in values[j]:
                 nc.vector.tensor_copy(placed[j][:].indirect(places), v[:])
-            nc.gpsimd.tensor_tensor(kept[:], kept[:], placed[j][:], ADD)
-            nc.sync.dma_start(out_v[:, j, :], kept[:])
+            parts = 2 if j == TILES - 2 else 1
+            for b in range(parts):
+                cols = slice(b * T // parts, (b + 1) * T // parts)
+                nc.gpsimd.tensor_tensor(kept[j][:, cols], kept[j][:, cols], placed[j][:, cols], ADD)
+                nc.sync.dma_start(out_v[:, j, cols], kept[j][:, cols])
 
         for v, places in values[3]:
             nc.vector.tensor_copy(placed[0][:].indirect(places), v[:])
-        last = keep.tile([P, T], F32, name="last", tag="grouped0", align_bytes=64)
+        last = keep.tile([P, T], F32, name="last")
         for b in range(T // BANK):
             cols = slice(b * BANK, (b + 1) * BANK)
-            nc.vector.tensor_tensor(last[:, cols], kept3[b][:], placed[0][:, cols], ADD)
+            nc.vector.tensor_tensor(last[:, cols], bank[6 + b][:], placed[0][:, cols], ADD)
             nc.sync.dma_start(out_v[:, 3, cols], last[:, cols])

@@ -38,7 +38,7 @@ def tile_attend_headwrite_kernel(tc, emb_words, emb_scales, wv, old, retain, off
 
         slot_list = keep.tile([P, I // 16], U16, name="slot_list")
         place_list = keep.tile([P, I // 16], U16, name="place_list")
-        zeros = keep.tile([P, P], F32, name="zeros", tag="zeros_words")
+        zeros = keep.tile([P, P], F32, name="zeros", tag="zeros_words", align_bytes=64)
         scales = keep.tile([P, U], U8, name="scales", tag="scales_old0")
         w_raw = keep.tile([P, PACK, E], F32, name="w_raw", tag="w_old0")
         retain_rows = keep.tile([P, P], F32, name="retain_rows")
@@ -59,7 +59,7 @@ def tile_attend_headwrite_kernel(tc, emb_words, emb_scales, wv, old, retain, off
         nc.scalar.activation(ident[:], zeros[:], COPY)
         make_identity(nc, ident[:], nomemset=True)
         nc.sync.dma_start(w_raw[:, 2:4, :], wv_v[:, 2:4, :])
-        words = keep.tile([P, 2 * U], U8, name="words", tag="zeros_words")
+        words = keep.tile([P, 2 * U], U8, name="words", tag="zeros_words", align_bytes=64)
         nc.sync.dma_start(words[:].bitcast(I32), emb_words[0].bitcast(I32))
         nc.sync.dma_start(retain_rows[0:BLOCKS, :], retain.rearrange("o (c p) -> (o c) p", p=P))
         for window in placed:
@@ -67,66 +67,71 @@ def tile_attend_headwrite_kernel(tc, emb_words, emb_scales, wv, old, retain, off
 
         got_words = keep.tile([P, 2 * I], U8, name="got_words", align_bytes=64)
         got_scales = keep.tile([P, I], U8, name="got_scales", align_bytes=64)
-        nc.vector.tensor_copy(got_scales[:], scales[:].indirect(slot_list[:]))
-
         w_by_col = w_raw[:].rearrange("p t (m j) -> p m j t", j=TILES)
         grouped = [
             keep.tile([P, 2, P, PACK], BF16, name="grouped%d" % g, tag="grouped%d" % g, align_bytes=64)
             for g in range(2)
         ]
-        nc.vector.tensor_copy(grouped[0][:].rearrange("p j m t -> p m j t"), w_by_col[:, :, 0:2, :])
-        nc.scalar.activation(grouped[1][:].rearrange("p j m t -> p m j t"), w_by_col[:, :, 2:4, :], COPY)
+        dealt = [g[:].rearrange("p j m t -> p m j t") for g in grouped]
+        for t in (slice(0, 2), slice(2, 4)):
+            nc.vector.tensor_copy(dealt[0][:, :, :, t], w_by_col[:, :, 0:2, t])
+            nc.scalar.activation(dealt[1][:, :, :, t], w_by_col[:, :, 2:4, t], COPY)
+            if t.start == 0:
+                nc.vector.tensor_copy(got_scales[:], scales[:].indirect(slot_list[:]))
 
-        codes = keep.tile([P, E], U32, name="codes", align_bytes=64)
         w_scales = keep.tile([P, E], U8, name="w_scales", align_bytes=64)
+        codes = []
 
-        def quantise(j0, j1):
+        def quantise(g, tag):
+            codes.append(keep.tile([P, 2 * P], U32, name="codes%d" % g, tag=tag, align_bytes=64))
             nc.vector.quantize_mx(
-                out=codes[:, j0 * P : j1 * P].bitcast(FP8X4),
-                scales=w_scales[:, j0 * P : j1 * P],
-                in_=grouped[j0 // 2][:, j0 % 2 : j0 % 2 + j1 - j0].rearrange("p j m t -> p (j m t)"),
+                out=codes[g][:].bitcast(FP8X4),
+                scales=w_scales[:, 2 * g * P : 2 * (g + 1) * P],
+                in_=grouped[g][:].rearrange("p j m t -> p (j m t)"),
             )
 
-        def project(j, i0, i1, acc):
-            nc.tensor.matmul_mx(
-                out=acc[:, 0 : i1 - i0],
-                lhsT=codes[:, j * P : (j + 1) * P].bitcast(FP8X4),
-                lhsT_scale=w_scales[:, j * P : (j + 1) * P],
-                rhs=got_words[:, 2 * i0 : 2 * i1].bitcast(FP4X4),
-                rhs_scale=got_scales[:, i0:i1],
-                start=True,
-                stop=True,
-            )
-            v = keep.tile([P, i1 - i0], F32, name="v%d_%d" % (j, i0))
-            nc.scalar.activation(v[:], acc[:, 0 : i1 - i0], COPY)
-            return v, place_list[:, i0 // 16 : i1 // 16]
+        def project(j, cuts, acc):
+            first, last = cuts[0], cuts[-1]
+            for i0, i1 in zip(cuts, cuts[1:]):
+                nc.tensor.matmul_mx(
+                    out=acc[:, i0 - first : i1 - first],
+                    lhsT=codes[j // 2][:, j % 2 * P : (j % 2 + 1) * P].bitcast(FP8X4),
+                    lhsT_scale=w_scales[:, j * P : (j + 1) * P],
+                    rhs=got_words[:, 2 * i0 : 2 * i1].bitcast(FP4X4),
+                    rhs_scale=got_scales[:, i0:i1],
+                    start=True,
+                    stop=True,
+                )
+            v = keep.tile([P, last - first], F32, name="v%d_%d" % (j, first))
+            nc.scalar.activation(v[:], acc[:, 0 : last - first], COPY)
+            return v, place_list[:, first // 16 : last // 16]
 
-        quantise(0, 2)
+        quantise(0, "codes0")
         for h in range(2):
             nc.vector.tensor_copy(
                 got_words[:, 2 * h * HALF : 2 * (h + 1) * HALF].bitcast(U16),
                 words[:].bitcast(U16).indirect(slot_list[:, h * HALF // 16 : (h + 1) * HALF // 16]),
             )
-        quantise(2, 4)
+        quantise(1, "zeros_words")
 
-        nc.tensor.transpose(bank[0][:, 0:P], retain_rows[:], ident[:])
+        pieces = [(j, project(j, (0, P), bank[j])) for j in range(2)]
+
+        nc.tensor.transpose(bank[5][:, 0:P], retain_rows[:], ident[:])
         retain_cols = keep.tile([P, BLOCKS], F32, name="retain_cols")
-        nc.scalar.activation(retain_cols[:], bank[0][:, 0:BLOCKS], COPY)
-
-        values = [[project(0, 0, HALF, bank[1]), project(0, HALF, I, bank[2])], [project(1, 0, I, bank[3])]]
-
+        nc.scalar.activation(retain_cols[:], bank[5][:, 0:BLOCKS], COPY)
         retain_all = keep.tile([P, T], F32, name="retain_all")
         for b in range(T // BANK):
-            spread = bank[1 + b]
+            spread = bank[6 + b]
             for c in range(BANK // P):
                 col = b * (BANK // P) + c
                 nc.tensor.transpose(
                     spread[:, c * P : (c + 1) * P], retain_cols[:, col : col + 1].to_broadcast([P, P]), ident[:]
                 )
             nc.scalar.activation(retain_all[:, b * BANK : (b + 1) * BANK], spread[:], COPY)
+            pieces.append((b, project(b, (P, HALF, I), bank[2 + b])))
 
-        values.append([project(2, 0, I, bank[0])])
-        values.append([project(3, 0, I, bank[4])])
+        pieces.append((2, project(2, (0, I), bank[4])))
+        pieces.append((3, project(3, (0, I), bank[5])))
 
         old0 = keep.tile([P, T], F32, name="old0", tag="scales_old0")
         nc.sync.dma_start(old0[:], old_v[:, 0, :])
@@ -136,7 +141,9 @@ def tile_attend_headwrite_kernel(tc, emb_words, emb_scales, wv, old, retain, off
 
         placed.append(keep.tile([P, T], F32, name="placed2", tag="grouped1", align_bytes=64))
         nc.gpsimd.memset(placed[2][:].bitcast(I32), 0)
-        nc.gpsimd.tensor_tensor(old0[:], old0[:], retain_all[:], MULT)
+        for b in range(T // BANK):
+            cols = slice(b * BANK, (b + 1) * BANK)
+            nc.gpsimd.tensor_tensor(old0[:, cols], old0[:, cols], retain_all[:, cols], MULT)
 
         kept = [old0]
         for j in range(1, TILES):
@@ -160,17 +167,17 @@ def tile_attend_headwrite_kernel(tc, emb_words, emb_scales, wv, old, retain, off
                 if j < TILES - 1:
                     nc.scalar.activation(kept[j][:, b * BANK : (b + 1) * BANK], back[:], COPY)
 
+        for j, (v, places) in pieces[:-1]:
+            nc.vector.tensor_copy(placed[j][:].indirect(places), v[:])
         for j in range(TILES - 1):
-            for v, places in values[j]:
-                nc.vector.tensor_copy(placed[j][:].indirect(places), v[:])
             parts = 2 if j == TILES - 2 else 1
             for b in range(parts):
                 cols = slice(b * T // parts, (b + 1) * T // parts)
                 nc.gpsimd.tensor_tensor(kept[j][:, cols], kept[j][:, cols], placed[j][:, cols], ADD)
                 nc.sync.dma_start(out_v[:, j, cols], kept[j][:, cols])
 
-        for v, places in values[3]:
-            nc.vector.tensor_copy(placed[0][:].indirect(places), v[:])
+        v, places = pieces[-1][1]
+        nc.vector.tensor_copy(placed[0][:].indirect(places), v[:])
         last = keep.tile([P, T], F32, name="last")
         for b in range(T // BANK):
             cols = slice(b * BANK, (b + 1) * BANK)

@@ -56,7 +56,7 @@ def tile_attend_headwrite_kernel(tc, emb_words, emb_scales, wv, old, retain, off
         for r in range(4):
             nc.sync.dma_start(scales[r:P:32, :].bitcast(I32), emb_scales[0, r:16:4, :].bitcast(I32))
         nc.vector.tensor_copy(retain_rows[:], w_raw[:, 3, 0:P])
-        nc.scalar.activation(ident[:], zeros[:], COPY)
+        nc.vector.tensor_copy(ident[:], zeros[:])
         make_identity(nc, ident[:], nomemset=True)
         nc.sync.dma_start(w_raw[:, 2:4, :], wv_v[:, 2:4, :])
         words = keep.tile([P, 2 * U], U8, name="words", tag="zeros_words", align_bytes=64)
@@ -179,7 +179,8 @@ def tile_attend_headwrite_kernel(tc, emb_words, emb_scales, wv, old, retain, off
         v, places = pieces[-1][1]
         nc.vector.tensor_copy(placed[0][:].indirect(places), v[:])
         last = keep.tile([P, T], F32, name="last")
-        for b in range(T // BANK):
-            cols = slice(b * BANK, (b + 1) * BANK)
-            nc.vector.tensor_tensor(last[:, cols], bank[6 + b][:], placed[0][:, cols], ADD)
+        for q in range(4):
+            cols = slice(q * HALF, (q + 1) * HALF)
+            in_bank = slice(q % 2 * HALF, (q % 2 + 1) * HALF)
+            nc.vector.tensor_tensor(last[:, cols], bank[6 + q // 2][:, in_bank], placed[0][:, cols], ADD)
             nc.sync.dma_start(out_v[:, 3, cols], last[:, cols])

@@ -39,7 +39,7 @@ def tile_attend_headwrite_kernel(tc, emb_words, emb_scales, wv, old, retain, off
         slot_list = keep.tile([P, I // 16], U16, name="slot_list")
         place_list = keep.tile([P, I // 16], U16, name="place_list")
         zeros = keep.tile([P, P], F32, name="zeros", tag="zeros_words", align_bytes=64)
-        scales = keep.tile([P, U], U8, name="scales", tag="scales_old0")
+        scales = keep.tile([P, U], U8, name="scales", tag="grouped0", align_bytes=64)
         w_raw = keep.tile([P, PACK, E], F32, name="w_raw", tag="w_old0")
         retain_rows = keep.tile([P, P], F32, name="retain_rows")
         ident = keep.tile([P, P], F32, name="ident")
@@ -47,18 +47,17 @@ def tile_attend_headwrite_kernel(tc, emb_words, emb_scales, wv, old, retain, off
 
         wv_v = wv.rearrange("(p t) e -> p t e", t=PACK)
         nc.sync.dma_start(slot_list[:], offs)
-        nc.sync.dma_start(w_raw[:, 0:2, :], wv_v[:, 0:2, :])
+        nc.sync.dma_start(w_raw[:, 0:1, :], wv_v[:, 0:1, :])
         nc.sync.dma_start(place_list[:], offs2)
 
         nc.vector.memset(w_raw[:, 3, 0:P], 0.0)
         nc.vector.memset(zeros[:], 0.0)
         nc.vector.memset(scales[:].bitcast(I32), 0)
-        for r in range(4):
-            nc.sync.dma_start(scales[r:P:32, :].bitcast(I32), emb_scales[0, r:16:4, :].bitcast(I32))
+        nc.sync.dma_start(scales[0:P:8, :].bitcast(I32), emb_scales[0].bitcast(I32))
         nc.vector.tensor_copy(retain_rows[:], w_raw[:, 3, 0:P])
         nc.vector.tensor_copy(ident[:], zeros[:])
         make_identity(nc, ident[:], nomemset=True)
-        nc.sync.dma_start(w_raw[:, 2:4, :], wv_v[:, 2:4, :])
+        nc.sync.dma_start(w_raw[:, 1:4, :], wv_v[:, 1:4, :])
         words = keep.tile([P, 2 * U], U8, name="words", tag="zeros_words", align_bytes=64)
         nc.sync.dma_start(words[:].bitcast(I32), emb_words[0].bitcast(I32))
         nc.sync.dma_start(retain_rows[0:BLOCKS, :], retain.rearrange("o (c p) -> (o c) p", p=P))
@@ -66,18 +65,21 @@ def tile_attend_headwrite_kernel(tc, emb_words, emb_scales, wv, old, retain, off
             nc.vector.memset(window[:].bitcast(I32), 0)
 
         got_words = keep.tile([P, 2 * I], U8, name="got_words", align_bytes=64)
+        got_rows = keep.tile([P, I], U8, name="got_rows")
         got_scales = keep.tile([P, I], U8, name="got_scales", align_bytes=64)
+        nc.vector.memset(got_scales[:].bitcast(I32), 0)
+        nc.vector.tensor_copy(got_rows[:], scales[:].indirect(slot_list[:]))
+        for r in range(4):
+            nc.sync.dma_start(got_scales[r:P:32, :].bitcast(I32), got_rows[8 * r : P : 32, :].bitcast(I32))
         w_by_col = w_raw[:].rearrange("p t (m j) -> p m j t", j=TILES)
         grouped = [
             keep.tile([P, 2, P, PACK], BF16, name="grouped%d" % g, tag="grouped%d" % g, align_bytes=64)
             for g in range(2)
         ]
         dealt = [g[:].rearrange("p j m t -> p m j t") for g in grouped]
-        for t in (slice(0, 2), slice(2, 4)):
+        for t in (slice(0, 1), slice(1, 4)):
             nc.vector.tensor_copy(dealt[0][:, :, :, t], w_by_col[:, :, 0:2, t])
             nc.scalar.activation(dealt[1][:, :, :, t], w_by_col[:, :, 2:4, t], COPY)
-            if t.start == 0:
-                nc.vector.tensor_copy(got_scales[:], scales[:].indirect(slot_list[:]))
 
         w_scales = keep.tile([P, E], U8, name="w_scales", align_bytes=64)
         codes = []
@@ -116,56 +118,46 @@ def tile_attend_headwrite_kernel(tc, emb_words, emb_scales, wv, old, retain, off
 
         pieces = [(j, project(j, (0, P), bank[j])) for j in range(2)]
 
-        nc.tensor.transpose(bank[5][:, 0:P], retain_rows[:], ident[:])
+        nc.tensor.transpose(bank[0][:, 0:P], retain_rows[:], ident[:])
         retain_cols = keep.tile([P, BLOCKS], F32, name="retain_cols")
-        nc.scalar.activation(retain_cols[:], bank[5][:, 0:BLOCKS], COPY)
-        retain_all = keep.tile([P, T], F32, name="retain_all")
-        for b in range(T // BANK):
-            spread = bank[6 + b]
-            for c in range(BANK // P):
-                col = b * (BANK // P) + c
-                nc.tensor.transpose(
-                    spread[:, c * P : (c + 1) * P], retain_cols[:, col : col + 1].to_broadcast([P, P]), ident[:]
-                )
-            nc.scalar.activation(retain_all[:, b * BANK : (b + 1) * BANK], spread[:], COPY)
-            pieces.append((b, project(b, (P, HALF, I), bank[2 + b])))
+        nc.scalar.activation(retain_cols[:], bank[0][:, 0:BLOCKS], COPY)
+        retain_all = keep.tile([P, BANK], F32, name="retain_all")
+        for c in range(BANK // P):
+            nc.tensor.transpose(
+                bank[6][:, c * P : (c + 1) * P], retain_cols[:, c : c + 1].to_broadcast([P, P]), ident[:]
+            )
+        nc.scalar.activation(retain_all[:], bank[6][:], COPY)
+        pieces.extend((j, project(j, (P, HALF, I), bank[2 + j])) for j in range(2))
 
         pieces.append((2, project(2, (0, I), bank[4])))
         pieces.append((3, project(3, (0, I), bank[5])))
 
-        old0 = keep.tile([P, T], F32, name="old0", tag="scales_old0")
-        nc.sync.dma_start(old0[:], old_v[:, 0, :])
-        old_rest = keep.tile([P, (TILES - 1) * T], F32, name="old_rest", tag="w_old0")
-        for j in range(1, TILES):
-            nc.sync.dma_start(old_rest[:, (j - 1) * T : j * T], old_v[:, j, :])
+        old_all = keep.tile([P, TILES * T], F32, name="old_all", tag="w_old0")
+        for j in range(TILES):
+            nc.sync.dma_start(old_all[:, j * T : (j + 1) * T], old_v[:, j, :])
 
         placed.append(keep.tile([P, T], F32, name="placed2", tag="grouped1", align_bytes=64))
         nc.gpsimd.memset(placed[2][:].bitcast(I32), 0)
-        for b in range(T // BANK):
-            cols = slice(b * BANK, (b + 1) * BANK)
-            nc.gpsimd.tensor_tensor(old0[:, cols], old0[:, cols], retain_all[:, cols], MULT)
+        nc.gpsimd.tensor_tensor(old_all[:, 0:BANK], old_all[:, 0:BANK], retain_all[:], MULT)
 
-        kept = [old0]
-        for j in range(1, TILES):
+        for step in range(1, TILES * T // BANK):
+            j, b = divmod(step, T // BANK)
+            turn = bank[step % 3]
+            back = bank[6 + b] if j == TILES - 1 else bank[3 + step % 3]
+            turned = keep.tile([P, BANK], F32, name="turned%d" % step)
+            for cc in range(4):
+                at = step * BANK + cc * P
+                nc.tensor.transpose(turn[:, cc * P : (cc + 1) * P], old_all[:, at : at + P], ident[:])
+            for cc in range(4):
+                c = 4 * b + cc
+                cols = slice(cc * P, (cc + 1) * P)
+                nc.scalar.activation(turned[:, cols], turn[:, cols], COPY, scale=retain_cols[:, c : c + 1])
+            for cc in range(4):
+                cols = slice(cc * P, (cc + 1) * P)
+                nc.tensor.transpose(back[:, cols], turned[:, cols], ident[:])
             if j < TILES - 1:
-                kept.append(keep.tile([P, T], F32, name="kept%d" % j))
-            for b in range(T // BANK):
-                step = 2 * (j - 1) + b
-                turn = bank[step % 3]
-                back = bank[6 + b] if j == TILES - 1 else bank[3 + step % 3]
-                turned = keep.tile([P, BANK], F32, name="turned%d" % step)
-                for cc in range(4):
-                    at = (j - 1) * T + b * BANK + cc * P
-                    nc.tensor.transpose(turn[:, cc * P : (cc + 1) * P], old_rest[:, at : at + P], ident[:])
-                for cc in range(4):
-                    c = 4 * b + cc
-                    cols = slice(cc * P, (cc + 1) * P)
-                    nc.scalar.activation(turned[:, cols], turn[:, cols], COPY, scale=retain_cols[:, c : c + 1])
-                for cc in range(4):
-                    cols = slice(cc * P, (cc + 1) * P)
-                    nc.tensor.transpose(back[:, cols], turned[:, cols], ident[:])
-                if j < TILES - 1:
-                    nc.scalar.activation(kept[j][:, b * BANK : (b + 1) * BANK], back[:], COPY)
+                nc.scalar.activation(old_all[:, step * BANK : (step + 1) * BANK], back[:], COPY)
+        kept = [old_all[:, j * T : (j + 1) * T] for j in range(TILES - 1)]
 
         for j, (v, places) in pieces[:-1]:
             nc.vector.tensor_copy(placed[j][:].indirect(places), v[:])

@@ -39,8 +39,8 @@ def tile_attend_headwrite_kernel(tc, emb_words, emb_scales, wv, old, retain, off
         slot_list = keep.tile([P, I // 16], U16, name="slot_list")
         place_list = keep.tile([P, I // 16], U16, name="place_list")
         zeros = keep.tile([P, P], F32, name="zeros", tag="zeros_words", align_bytes=64)
-        scales = keep.tile([P, U], U8, name="scales", tag="grouped0", align_bytes=64)
-        w_raw = keep.tile([P, PACK, E], F32, name="w_raw", tag="w_old0")
+        scales = keep.tile([P, U], U8, name="scales", tag="scales_old")
+        w_raw = keep.tile([P, PACK, E], F32, name="w_raw")
         retain_rows = keep.tile([P, P], F32, name="retain_rows")
         ident = keep.tile([P, P], F32, name="ident")
         placed = [keep.tile([P, T], F32, name="placed%d" % i) for i in range(2)]
@@ -50,14 +50,15 @@ def tile_attend_headwrite_kernel(tc, emb_words, emb_scales, wv, old, retain, off
         nc.sync.dma_start(w_raw[:, 0:1, :], wv_v[:, 0:1, :])
         nc.sync.dma_start(place_list[:], offs2)
 
-        nc.vector.memset(w_raw[:, 3, 0:P], 0.0)
+        nc.vector.memset(w_raw[:, 1:3, 0:P // 2], 0.0)
         nc.vector.memset(zeros[:], 0.0)
         nc.vector.memset(scales[:].bitcast(I32), 0)
         nc.sync.dma_start(scales[0:P:8, :].bitcast(I32), emb_scales[0].bitcast(I32))
-        nc.vector.tensor_copy(retain_rows[:], w_raw[:, 3, 0:P])
-        nc.vector.tensor_copy(ident[:], zeros[:])
+        nc.vector.tensor_copy(retain_rows[:].rearrange("p (a c) -> p a c", a=2), w_raw[:, 1:3, 0:P // 2])
+        nc.scalar.activation(ident[:], zeros[:], COPY)
         make_identity(nc, ident[:], nomemset=True)
-        nc.sync.dma_start(w_raw[:, 1:4, :], wv_v[:, 1:4, :])
+        nc.sync.dma_start(w_raw[:, 1:2, :], wv_v[:, 1:2, :])
+        nc.sync.dma_start(w_raw[:, 2:4, :], wv_v[:, 2:4, :])
         words = keep.tile([P, 2 * U], U8, name="words", tag="zeros_words", align_bytes=64)
         nc.sync.dma_start(words[:].bitcast(I32), emb_words[0].bitcast(I32))
         nc.sync.dma_start(retain_rows[0:BLOCKS, :], retain.rearrange("o (c p) -> (o c) p", p=P))
@@ -71,15 +72,17 @@ def tile_attend_headwrite_kernel(tc, emb_words, emb_scales, wv, old, retain, off
         nc.vector.tensor_copy(got_rows[:], scales[:].indirect(slot_list[:]))
         for r in range(4):
             nc.sync.dma_start(got_scales[r:P:32, :].bitcast(I32), got_rows[8 * r : P : 32, :].bitcast(I32))
+
         w_by_col = w_raw[:].rearrange("p t (m j) -> p m j t", j=TILES)
         grouped = [
             keep.tile([P, 2, P, PACK], BF16, name="grouped%d" % g, tag="grouped%d" % g, align_bytes=64)
             for g in range(2)
         ]
         dealt = [g[:].rearrange("p j m t -> p m j t") for g in grouped]
-        for t in (slice(0, 1), slice(1, 4)):
-            nc.vector.tensor_copy(dealt[0][:, :, :, t], w_by_col[:, :, 0:2, t])
-            nc.scalar.activation(dealt[1][:, :, :, t], w_by_col[:, :, 2:4, t], COPY)
+        nc.scalar.activation(dealt[0][:, :, :, 0:2], w_by_col[:, :, 0:2, 0:2], COPY)
+        nc.scalar.activation(dealt[1][:, :, :, 0:2], w_by_col[:, :, 2:4, 0:2], COPY)
+        nc.vector.tensor_copy(dealt[0][:, :, :, 2:4], w_by_col[:, :, 0:2, 2:4])
+        nc.scalar.activation(dealt[1][:, :, :, 2:4], w_by_col[:, :, 2:4, 2:4], COPY)
 
         w_scales = keep.tile([P, E], U8, name="w_scales", align_bytes=64)
         codes = []
@@ -121,29 +124,30 @@ def tile_attend_headwrite_kernel(tc, emb_words, emb_scales, wv, old, retain, off
         nc.tensor.transpose(bank[0][:, 0:P], retain_rows[:], ident[:])
         retain_cols = keep.tile([P, BLOCKS], F32, name="retain_cols")
         nc.scalar.activation(retain_cols[:], bank[0][:, 0:BLOCKS], COPY)
-        retain_all = keep.tile([P, BANK], F32, name="retain_all")
-        for c in range(BANK // P):
-            nc.tensor.transpose(
-                bank[6][:, c * P : (c + 1) * P], retain_cols[:, c : c + 1].to_broadcast([P, P]), ident[:]
-            )
-        nc.scalar.activation(retain_all[:], bank[6][:], COPY)
+        retain_all = keep.tile([P, T], F32, name="retain_all")
+        for b in range(T // BANK):
+            for c in range(BANK // P):
+                col = b * (BANK // P) + c
+                nc.tensor.transpose(
+                    bank[6 + b][:, c * P : (c + 1) * P], retain_cols[:, col : col + 1].to_broadcast([P, P]), ident[:]
+                )
+            nc.scalar.activation(retain_all[:, b * BANK : (b + 1) * BANK], bank[6 + b][:], COPY)
         pieces.extend((j, project(j, (P, HALF, I), bank[2 + j])) for j in range(2))
 
-        pieces.append((2, project(2, (0, I), bank[4])))
-        pieces.append((3, project(3, (0, I), bank[5])))
-
-        old_all = keep.tile([P, TILES * T], F32, name="old_all", tag="w_old0")
+        old_all = keep.tile([P, TILES * T], F32, name="old_all", tag="scales_old")
         for j in range(TILES):
             nc.sync.dma_start(old_all[:, j * T : (j + 1) * T], old_v[:, j, :])
 
         placed.append(keep.tile([P, T], F32, name="placed2", tag="grouped1", align_bytes=64))
         nc.gpsimd.memset(placed[2][:].bitcast(I32), 0)
-        nc.gpsimd.tensor_tensor(old_all[:, 0:BANK], old_all[:, 0:BANK], retain_all[:], MULT)
+        for b in range(T // BANK):
+            cols = slice(b * BANK, (b + 1) * BANK)
+            nc.gpsimd.tensor_tensor(old_all[:, cols], old_all[:, cols], retain_all[:, cols], MULT)
 
-        for step in range(1, TILES * T // BANK):
+        for step in range(T // BANK, TILES * T // BANK):
             j, b = divmod(step, T // BANK)
             turn = bank[step % 3]
-            back = bank[6 + b] if j == TILES - 1 else bank[3 + step % 3]
+            back = bank[6 + b] if j == TILES - 1 else bank[3 + step % 2]
             turned = keep.tile([P, BANK], F32, name="turned%d" % step)
             for cc in range(4):
                 at = step * BANK + cc * P
@@ -157,6 +161,8 @@ def tile_attend_headwrite_kernel(tc, emb_words, emb_scales, wv, old, retain, off
                 nc.tensor.transpose(back[:, cols], turned[:, cols], ident[:])
             if j < TILES - 1:
                 nc.scalar.activation(old_all[:, step * BANK : (step + 1) * BANK], back[:], COPY)
+            if (j, b) in ((1, 1), (2, 0)):
+                pieces.append((j + 1, project(j + 1, (0, I), bank[5])))
         kept = [old_all[:, j * T : (j + 1) * T] for j in range(TILES - 1)]
 
         for j, (v, places) in pieces[:-1]:
@@ -170,7 +176,7 @@ def tile_attend_headwrite_kernel(tc, emb_words, emb_scales, wv, old, retain, off
 
         v, places = pieces[-1][1]
         nc.vector.tensor_copy(placed[0][:].indirect(places), v[:])
-        last = keep.tile([P, T], F32, name="last")
+        last = keep.tile([P, T], F32, name="last", tag="grouped1", align_bytes=64)
         for q in range(4):
             cols = slice(q * HALF, (q + 1) * HALF)
             in_bank = slice(q % 2 * HALF, (q % 2 + 1) * HALF)

@@ -46,8 +46,8 @@ def tile_attend_headwrite_kernel(tc, emb_words, emb_scales, wv, old, retain, off
         placed = [keep.tile([P, T], F32, name="placed%d" % i) for i in range(2)]
 
         wv_v = wv.rearrange("(p t) e -> p t e", t=PACK)
-        nc.sync.dma_start(slot_list[:], offs)
         nc.sync.dma_start(w_raw[:, 0:1, :], wv_v[:, 0:1, :])
+        nc.sync.dma_start(slot_list[:], offs)
         nc.sync.dma_start(place_list[:], offs2)
 
         nc.vector.memset(w_raw[:, 1:3, 0:P // 2], 0.0)
@@ -57,11 +57,11 @@ def tile_attend_headwrite_kernel(tc, emb_words, emb_scales, wv, old, retain, off
         nc.vector.tensor_copy(retain_rows[:].rearrange("p (a c) -> p a c", a=2), w_raw[:, 1:3, 0:P // 2])
         nc.scalar.activation(ident[:], zeros[:], COPY)
         make_identity(nc, ident[:], nomemset=True)
+        nc.sync.dma_start(retain_rows[0:BLOCKS, :], retain.rearrange("o (c p) -> (o c) p", p=P))
         nc.sync.dma_start(w_raw[:, 1:2, :], wv_v[:, 1:2, :])
         nc.sync.dma_start(w_raw[:, 2:4, :], wv_v[:, 2:4, :])
         words = keep.tile([P, 2 * U], U8, name="words", tag="zeros_words", align_bytes=64)
         nc.sync.dma_start(words[:].bitcast(I32), emb_words[0].bitcast(I32))
-        nc.sync.dma_start(retain_rows[0:BLOCKS, :], retain.rearrange("o (c p) -> (o c) p", p=P))
         for window in placed:
             nc.vector.memset(window[:].bitcast(I32), 0)
 
@@ -69,9 +69,27 @@ def tile_attend_headwrite_kernel(tc, emb_words, emb_scales, wv, old, retain, off
         got_rows = keep.tile([P, I], U8, name="got_rows")
         got_scales = keep.tile([P, I], U8, name="got_scales", align_bytes=64)
         nc.vector.memset(got_scales[:].bitcast(I32), 0)
-        nc.vector.tensor_copy(got_rows[:], scales[:].indirect(slot_list[:]))
-        for r in range(4):
-            nc.sync.dma_start(got_scales[r:P:32, :].bitcast(I32), got_rows[8 * r : P : 32, :].bitcast(I32))
+        for h in range(2):
+            cols = slice(h * HALF, (h + 1) * HALF)
+            nc.vector.tensor_copy(
+                got_rows[:, cols], scales[:].indirect(slot_list[:, h * HALF // 16 : (h + 1) * HALF // 16])
+            )
+            for r in range(4):
+                nc.sync.dma_start(
+                    got_scales[r:P:32, cols].bitcast(I32), got_rows[8 * r : P : 32, cols].bitcast(I32)
+                )
+
+        nc.tensor.transpose(bank[5][:, 0:P], retain_rows[:], ident[:])
+        retain_cols = keep.tile([P, BLOCKS], F32, name="retain_cols")
+        nc.scalar.activation(retain_cols[:], bank[5][:, 0:BLOCKS], COPY)
+        retain_all = keep.tile([P, T], F32, name="retain_all")
+        for b in range(T // BANK):
+            for c in range(BANK // P):
+                col = b * (BANK // P) + c
+                nc.tensor.transpose(
+                    bank[6 + b][:, c * P : (c + 1) * P], retain_cols[:, col : col + 1].to_broadcast([P, P]), ident[:]
+                )
+            nc.scalar.activation(retain_all[:, b * BANK : (b + 1) * BANK], bank[6 + b][:], COPY)
 
         w_by_col = w_raw[:].rearrange("p t (m j) -> p m j t", j=TILES)
         grouped = [
@@ -79,7 +97,7 @@ def tile_attend_headwrite_kernel(tc, emb_words, emb_scales, wv, old, retain, off
             for g in range(2)
         ]
         dealt = [g[:].rearrange("p j m t -> p m j t") for g in grouped]
-        nc.scalar.activation(dealt[0][:, :, :, 0:2], w_by_col[:, :, 0:2, 0:2], COPY)
+        nc.vector.tensor_copy(dealt[0][:, :, :, 0:2], w_by_col[:, :, 0:2, 0:2])
         nc.scalar.activation(dealt[1][:, :, :, 0:2], w_by_col[:, :, 2:4, 0:2], COPY)
         nc.vector.tensor_copy(dealt[0][:, :, :, 2:4], w_by_col[:, :, 0:2, 2:4])
         nc.scalar.activation(dealt[1][:, :, :, 2:4], w_by_col[:, :, 2:4, 2:4], COPY)
@@ -119,20 +137,11 @@ def tile_attend_headwrite_kernel(tc, emb_words, emb_scales, wv, old, retain, off
             )
         quantise(1, "zeros_words")
 
-        pieces = [(j, project(j, (0, P), bank[j])) for j in range(2)]
+        pieces = [(1, project(1, (0, P), bank[0])), (0, project(0, (0, HALF), bank[1]))]
+        pieces.append((1, project(1, (P, HALF), bank[2])))
 
-        nc.tensor.transpose(bank[0][:, 0:P], retain_rows[:], ident[:])
-        retain_cols = keep.tile([P, BLOCKS], F32, name="retain_cols")
-        nc.scalar.activation(retain_cols[:], bank[0][:, 0:BLOCKS], COPY)
-        retain_all = keep.tile([P, T], F32, name="retain_all")
-        for b in range(T // BANK):
-            for c in range(BANK // P):
-                col = b * (BANK // P) + c
-                nc.tensor.transpose(
-                    bank[6 + b][:, c * P : (c + 1) * P], retain_cols[:, col : col + 1].to_broadcast([P, P]), ident[:]
-                )
-            nc.scalar.activation(retain_all[:, b * BANK : (b + 1) * BANK], bank[6 + b][:], COPY)
-        pieces.extend((j, project(j, (P, HALF, I), bank[2 + j])) for j in range(2))
+        pieces.extend((j, project(j, (HALF, I), bank[3 + j])) for j in range(2))
+        pieces.append((2, project(2, (0, I), bank[5])))
 
         old_all = keep.tile([P, TILES * T], F32, name="old_all", tag="scales_old")
         for j in range(TILES):
@@ -161,8 +170,8 @@ def tile_attend_headwrite_kernel(tc, emb_words, emb_scales, wv, old, retain, off
                 nc.tensor.transpose(back[:, cols], turned[:, cols], ident[:])
             if j < TILES - 1:
                 nc.scalar.activation(old_all[:, step * BANK : (step + 1) * BANK], back[:], COPY)
-            if (j, b) in ((1, 1), (2, 0)):
-                pieces.append((j + 1, project(j + 1, (0, I), bank[5])))
+            if (j, b) == (1, 1):
+                pieces.append((3, project(3, (0, I), bank[5])))
         kept = [old_all[:, j * T : (j + 1) * T] for j in range(TILES - 1)]
 
         for j, (v, places) in pieces[:-1]:

@@ -30,6 +30,7 @@ def tile_attend_headwrite_kernel(tc, emb_words, emb_scales, wv, old, retain, off
     nc = tc.nc
     with ExitStack() as ctx:
         keep = ctx.enter_context(tc.tile_pool(name="keep", bufs=1))
+        laid = ctx.enter_context(tc.tile_pool(name="laid", bufs=1))
         psum = ctx.enter_context(tc.psum_pool(name="psum", bufs=1))
         bank = [psum.tile([P, BANK], F32, name="bank%d" % b) for b in range(8)]
 
@@ -38,32 +39,33 @@ def tile_attend_headwrite_kernel(tc, emb_words, emb_scales, wv, old, retain, off
 
         slot_list = keep.tile([P, I // 16], U16, name="slot_list")
         place_list = keep.tile([P, I // 16], U16, name="place_list")
-        zeros = keep.tile([P, P], F32, name="zeros", tag="zeros_words", align_bytes=64)
+        zeros = laid.tile([P, P], F32, name="zeros", offset=2 * U - 2 * P)
         scales = keep.tile([P, U], U8, name="scales", tag="scales_old")
-        w_raw = keep.tile([P, PACK, E], F32, name="w_raw")
-        retain_rows = keep.tile([P, P], F32, name="retain_rows")
+        w_raw = keep.tile([P, PACK * E], F32, name="w_raw")
+        retain_rows = keep.tile([P, P], F32, name="retain_rows", tag="grouped1", align_bytes=64)
         ident = keep.tile([P, P], F32, name="ident")
-        placed = [keep.tile([P, T], F32, name="placed%d" % i) for i in range(2)]
 
-        wv_v = wv.rearrange("(p t) e -> p t e", t=PACK)
-        nc.sync.dma_start(w_raw[:, 0:1, :], wv_v[:, 0:1, :])
+        wv_v = wv.rearrange("(p t) e -> p (t e)", t=PACK)
+        early, pair = 3 * E // 2, 2 * E
+        scratch = w_raw[:, pair - P // 2 : pair + P // 2]
+        nc.sync.dma_start(w_raw[:, 0:early], wv_v[:, 0:early])
         nc.sync.dma_start(slot_list[:], offs)
         nc.sync.dma_start(place_list[:], offs2)
 
-        nc.vector.memset(w_raw[:, 1:3, 0:P // 2], 0.0)
-        nc.vector.memset(zeros[:], 0.0)
+        nc.vector.memset(scratch, 0.0)
         nc.vector.memset(scales[:].bitcast(I32), 0)
         nc.sync.dma_start(scales[0:P:8, :].bitcast(I32), emb_scales[0].bitcast(I32))
-        nc.vector.tensor_copy(retain_rows[:].rearrange("p (a c) -> p a c", a=2), w_raw[:, 1:3, 0:P // 2])
+        nc.vector.tensor_copy(retain_rows[:], scratch)
+        nc.vector.memset(zeros[:], 0.0)
         nc.scalar.activation(ident[:], zeros[:], COPY)
         make_identity(nc, ident[:], nomemset=True)
         nc.sync.dma_start(retain_rows[0:BLOCKS, :], retain.rearrange("o (c p) -> (o c) p", p=P))
-        nc.sync.dma_start(w_raw[:, 1:2, :], wv_v[:, 1:2, :])
-        nc.sync.dma_start(w_raw[:, 2:4, :], wv_v[:, 2:4, :])
-        words = keep.tile([P, 2 * U], U8, name="words", tag="zeros_words", align_bytes=64)
+        nc.sync.dma_start(w_raw[:, early:pair], wv_v[:, early:pair])
+        nc.sync.dma_start(w_raw[:, pair:], wv_v[:, pair:])
+        words = laid.tile([P, 2 * U], U8, name="words", offset=0)
         nc.sync.dma_start(words[:].bitcast(I32), emb_words[0].bitcast(I32))
-        for window in placed:
-            nc.vector.memset(window[:].bitcast(I32), 0)
+        placed = [laid.tile([P, T], F32, name="placed0", offset=2 * U)]
+        nc.gpsimd.memset(placed[0][:].bitcast(I32), 0)
 
         got_words = keep.tile([P, 2 * I], U8, name="got_words", align_bytes=64)
         got_rows = keep.tile([P, I], U8, name="got_rows")
@@ -82,22 +84,14 @@ def tile_attend_headwrite_kernel(tc, emb_words, emb_scales, wv, old, retain, off
         nc.tensor.transpose(bank[5][:, 0:P], retain_rows[:], ident[:])
         retain_cols = keep.tile([P, BLOCKS], F32, name="retain_cols")
         nc.scalar.activation(retain_cols[:], bank[5][:, 0:BLOCKS], COPY)
-        retain_all = keep.tile([P, T], F32, name="retain_all")
-        for b in range(T // BANK):
-            for c in range(BANK // P):
-                col = b * (BANK // P) + c
-                nc.tensor.transpose(
-                    bank[6 + b][:, c * P : (c + 1) * P], retain_cols[:, col : col + 1].to_broadcast([P, P]), ident[:]
-                )
-            nc.scalar.activation(retain_all[:, b * BANK : (b + 1) * BANK], bank[6 + b][:], COPY)
 
-        w_by_col = w_raw[:].rearrange("p t (m j) -> p m j t", j=TILES)
+        w_by_col = w_raw[:].rearrange("p (t m j) -> p m j t", t=PACK, j=TILES)
         grouped = [
             keep.tile([P, 2, P, PACK], BF16, name="grouped%d" % g, tag="grouped%d" % g, align_bytes=64)
             for g in range(2)
         ]
         dealt = [g[:].rearrange("p j m t -> p m j t") for g in grouped]
-        nc.vector.tensor_copy(dealt[0][:, :, :, 0:2], w_by_col[:, :, 0:2, 0:2])
+        nc.scalar.activation(dealt[0][:, :, :, 0:2], w_by_col[:, :, 0:2, 0:2], COPY)
         nc.scalar.activation(dealt[1][:, :, :, 0:2], w_by_col[:, :, 2:4, 0:2], COPY)
         nc.vector.tensor_copy(dealt[0][:, :, :, 2:4], w_by_col[:, :, 0:2, 2:4])
         nc.scalar.activation(dealt[1][:, :, :, 2:4], w_by_col[:, :, 2:4, 2:4], COPY)
@@ -105,8 +99,8 @@ def tile_attend_headwrite_kernel(tc, emb_words, emb_scales, wv, old, retain, off
         w_scales = keep.tile([P, E], U8, name="w_scales", align_bytes=64)
         codes = []
 
-        def quantise(g, tag):
-            codes.append(keep.tile([P, 2 * P], U32, name="codes%d" % g, tag=tag, align_bytes=64))
+        def quantise(g, at):
+            codes.append(laid.tile([P, 2 * P], U32, name="codes%d" % g, offset=at, align_bytes=64))
             nc.vector.quantize_mx(
                 out=codes[g][:].bitcast(FP8X4),
                 scales=w_scales[:, 2 * g * P : 2 * (g + 1) * P],
@@ -129,16 +123,27 @@ def tile_attend_headwrite_kernel(tc, emb_words, emb_scales, wv, old, retain, off
             nc.scalar.activation(v[:], acc[:, 0 : last - first], COPY)
             return v, place_list[:, first // 16 : last // 16]
 
-        quantise(0, "codes0")
+        quantise(0, 2 * U + 4 * T)
+        placed.append(keep.tile([P, T], F32, name="placed1", tag="grouped0", align_bytes=64))
+        nc.gpsimd.memset(placed[1][:].bitcast(I32), 0)
         for h in range(2):
             nc.vector.tensor_copy(
                 got_words[:, 2 * h * HALF : 2 * (h + 1) * HALF].bitcast(U16),
                 words[:].bitcast(U16).indirect(slot_list[:, h * HALF // 16 : (h + 1) * HALF // 16]),
             )
-        quantise(1, "zeros_words")
+        quantise(1, 0)
 
         pieces = [(1, project(1, (0, P), bank[0])), (0, project(0, (0, HALF), bank[1]))]
         pieces.append((1, project(1, (P, HALF), bank[2])))
+
+        retain_all = keep.tile([P, T], F32, name="retain_all")
+        for b in range(T // BANK):
+            for c in range(BANK // P):
+                col = b * (BANK // P) + c
+                nc.tensor.transpose(
+                    bank[b][:, c * P : (c + 1) * P], retain_cols[:, col : col + 1].to_broadcast([P, P]), ident[:]
+                )
+            nc.scalar.activation(retain_all[:, b * BANK : (b + 1) * BANK], bank[b][:], COPY)
 
         pieces.extend((j, project(j, (HALF, I), bank[3 + j])) for j in range(2))
         pieces.append((2, project(2, (0, I), bank[5])))

@@ -24,6 +24,7 @@ TILES = E // P
 BANK = 512
 BLOCKS = T // P
 HALF = I // 2
+ROWS = K // 32
 
 
 def tile_attend_headwrite_kernel(tc, emb_words, emb_scales, wv, old, retain, offs, offs2, out):
@@ -39,51 +40,35 @@ def tile_attend_headwrite_kernel(tc, emb_words, emb_scales, wv, old, retain, off
 
         slot_list = keep.tile([P, I // 16], U16, name="slot_list")
         place_list = keep.tile([P, I // 16], U16, name="place_list")
-        zeros = laid.tile([P, P], F32, name="zeros", offset=2 * U - 2 * P)
         scales = keep.tile([P, U], U8, name="scales", tag="scales_old")
         w_raw = keep.tile([P, PACK * E], F32, name="w_raw")
-        retain_rows = keep.tile([P, P], F32, name="retain_rows", tag="grouped1", align_bytes=64)
+        words = laid.tile([P, 2 * U], U8, name="words", offset=0)
+        retain_rows = keep.tile([P, P], F32, name="retain_rows")
         ident = keep.tile([P, P], F32, name="ident")
 
-        wv_v = wv.rearrange("(p t) e -> p (t e)", t=PACK)
-        early, pair = 3 * E // 2, 2 * E
-        scratch = w_raw[:, pair - P // 2 : pair + P // 2]
-        nc.sync.dma_start(w_raw[:, 0:early], wv_v[:, 0:early])
+        nc.sync.dma_start(scales[P - ROWS : P, :].bitcast(I32), emb_scales[0].bitcast(I32))
         nc.sync.dma_start(slot_list[:], offs)
-        nc.sync.dma_start(place_list[:], offs2)
-
-        nc.vector.memset(scratch, 0.0)
-        nc.vector.memset(scales[:].bitcast(I32), 0)
-        nc.sync.dma_start(scales[0:P:8, :].bitcast(I32), emb_scales[0].bitcast(I32))
-        nc.vector.tensor_copy(retain_rows[:], scratch)
-        nc.vector.memset(zeros[:], 0.0)
-        nc.scalar.activation(ident[:], zeros[:], COPY)
-        make_identity(nc, ident[:], nomemset=True)
-        nc.sync.dma_start(retain_rows[0:BLOCKS, :], retain.rearrange("o (c p) -> (o c) p", p=P))
-        nc.sync.dma_start(w_raw[:, early:pair], wv_v[:, early:pair])
-        nc.sync.dma_start(w_raw[:, pair:], wv_v[:, pair:])
-        words = laid.tile([P, 2 * U], U8, name="words", offset=0)
+        nc.sync.dma_start(w_raw[:], wv.rearrange("(p t) e -> p (t e)", t=PACK))
         nc.sync.dma_start(words[:].bitcast(I32), emb_words[0].bitcast(I32))
-        placed = [laid.tile([P, T], F32, name="placed0", offset=2 * U)]
-        nc.gpsimd.memset(placed[0][:].bitcast(I32), 0)
+        nc.sync.dma_start(place_list[:], offs2)
 
         got_words = keep.tile([P, 2 * I], U8, name="got_words", align_bytes=64)
         got_rows = keep.tile([P, I], U8, name="got_rows")
         got_scales = keep.tile([P, I], U8, name="got_scales", align_bytes=64)
+        placed = [keep.tile([P, T], F32, name="placed0")]
+        nc.vector.memset(scales[0 : P - ROWS, :].bitcast(I32), 0)
         nc.vector.memset(got_scales[:].bitcast(I32), 0)
-        for h in range(2):
-            cols = slice(h * HALF, (h + 1) * HALF)
-            nc.vector.tensor_copy(
-                got_rows[:, cols], scales[:].indirect(slot_list[:, h * HALF // 16 : (h + 1) * HALF // 16])
-            )
-            for r in range(4):
-                nc.sync.dma_start(
-                    got_scales[r:P:32, cols].bitcast(I32), got_rows[8 * r : P : 32, cols].bitcast(I32)
-                )
+        nc.vector.memset(retain_rows[:], 0.0)
+        nc.sync.dma_start(retain_rows[0:BLOCKS, :], retain.rearrange("o (c p) -> (o c) p", p=P))
+        nc.vector.memset(placed[0][:].bitcast(I32), 0)
+        make_identity(nc, ident[:])
 
-        nc.tensor.transpose(bank[5][:, 0:P], retain_rows[:], ident[:])
-        retain_cols = keep.tile([P, BLOCKS], F32, name="retain_cols")
-        nc.scalar.activation(retain_cols[:], bank[5][:, 0:BLOCKS], COPY)
+        nc.vector.tensor_copy(got_rows[:], scales[:].indirect(slot_list[:]))
+        for r in range(4):
+            nc.sync.dma_start(got_scales[r:P:32, :].bitcast(I32), got_rows[P - ROWS + r : P : 4, :].bitcast(I32))
+        old_all = keep.tile([P, TILES * T], F32, name="old_all", tag="scales_old")
+        for j in range(TILES):
+            nc.sync.dma_start(old_all[:, j * T : (j + 1) * T], old_v[:, j, :])
 
         w_by_col = w_raw[:].rearrange("p (t m j) -> p m j t", t=PACK, j=TILES)
         grouped = [
@@ -91,10 +76,8 @@ def tile_attend_headwrite_kernel(tc, emb_words, emb_scales, wv, old, retain, off
             for g in range(2)
         ]
         dealt = [g[:].rearrange("p j m t -> p m j t") for g in grouped]
-        nc.scalar.activation(dealt[0][:, :, :, 0:2], w_by_col[:, :, 0:2, 0:2], COPY)
-        nc.scalar.activation(dealt[1][:, :, :, 0:2], w_by_col[:, :, 2:4, 0:2], COPY)
-        nc.vector.tensor_copy(dealt[0][:, :, :, 2:4], w_by_col[:, :, 0:2, 2:4])
-        nc.scalar.activation(dealt[1][:, :, :, 2:4], w_by_col[:, :, 2:4, 2:4], COPY)
+        nc.vector.tensor_copy(dealt[0], w_by_col[:, :, 0:2, :])
+        nc.scalar.activation(dealt[1], w_by_col[:, :, 2:4, :], COPY)
 
         w_scales = keep.tile([P, E], U8, name="w_scales", align_bytes=64)
         codes = []
@@ -123,7 +106,7 @@ def tile_attend_headwrite_kernel(tc, emb_words, emb_scales, wv, old, retain, off
             nc.scalar.activation(v[:], acc[:, 0 : last - first], COPY)
             return v, place_list[:, first // 16 : last // 16]
 
-        quantise(0, 2 * U + 4 * T)
+        quantise(0, 2 * U)
         placed.append(keep.tile([P, T], F32, name="placed1", tag="grouped0", align_bytes=64))
         nc.gpsimd.memset(placed[1][:].bitcast(I32), 0)
         for h in range(2):
@@ -133,9 +116,13 @@ def tile_attend_headwrite_kernel(tc, emb_words, emb_scales, wv, old, retain, off
             )
         quantise(1, 0)
 
-        pieces = [(1, project(1, (0, P), bank[0])), (0, project(0, (0, HALF), bank[1]))]
-        pieces.append((1, project(1, (P, HALF), bank[2])))
+        pieces = [(0, project(0, (0, P), bank[0])), (1, project(1, (0, HALF), bank[1]))]
+        pieces.append((0, project(0, (P, HALF, I), bank[2])))
+        pieces.append((1, project(1, (HALF, I), bank[3])))
 
+        nc.tensor.transpose(bank[0][:, 0:P], retain_rows[:], ident[:])
+        retain_cols = keep.tile([P, BLOCKS], F32, name="retain_cols")
+        nc.scalar.activation(retain_cols[:], bank[0][:, 0:BLOCKS], COPY)
         retain_all = keep.tile([P, T], F32, name="retain_all")
         for b in range(T // BANK):
             for c in range(BANK // P):
@@ -145,12 +132,7 @@ def tile_attend_headwrite_kernel(tc, emb_words, emb_scales, wv, old, retain, off
                 )
             nc.scalar.activation(retain_all[:, b * BANK : (b + 1) * BANK], bank[b][:], COPY)
 
-        pieces.extend((j, project(j, (HALF, I), bank[3 + j])) for j in range(2))
         pieces.append((2, project(2, (0, I), bank[5])))
-
-        old_all = keep.tile([P, TILES * T], F32, name="old_all", tag="scales_old")
-        for j in range(TILES):
-            nc.sync.dma_start(old_all[:, j * T : (j + 1) * T], old_v[:, j, :])
 
         placed.append(keep.tile([P, T], F32, name="placed2", tag="grouped1", align_bytes=64))
         nc.gpsimd.memset(placed[2][:].bitcast(I32), 0)

@@ -48,7 +48,9 @@ def tile_attend_headwrite_kernel(tc, emb_words, emb_scales, wv, old, retain, off
 
         nc.sync.dma_start(scales[P - ROWS : P, :].bitcast(I32), emb_scales[0].bitcast(I32))
         nc.sync.dma_start(slot_list[:], offs)
-        nc.sync.dma_start(w_raw[:], wv.rearrange("(p t) e -> p (t e)", t=PACK))
+        wv_v = wv.rearrange("(p t) e -> p (t e)", t=PACK)
+        for rows in (slice(0, 2 * E), slice(2 * E, 4 * E)):
+            nc.sync.dma_start(w_raw[:, rows], wv_v[:, rows])
         nc.sync.dma_start(words[:].bitcast(I32), emb_words[0].bitcast(I32))
         nc.sync.dma_start(place_list[:], offs2)
 
@@ -76,8 +78,9 @@ def tile_attend_headwrite_kernel(tc, emb_words, emb_scales, wv, old, retain, off
             for g in range(2)
         ]
         dealt = [g[:].rearrange("p j m t -> p m j t") for g in grouped]
-        nc.vector.tensor_copy(dealt[0], w_by_col[:, :, 0:2, :])
-        nc.scalar.activation(dealt[1], w_by_col[:, :, 2:4, :], COPY)
+        for rows in (slice(0, 2), slice(2, 4)):
+            nc.vector.tensor_copy(dealt[0][:, :, :, rows], w_by_col[:, :, 0:2, rows])
+            nc.scalar.activation(dealt[1][:, :, :, rows], w_by_col[:, :, 2:4, rows], COPY)
 
         w_scales = keep.tile([P, E], U8, name="w_scales", align_bytes=64)
         codes = []

@@ -78,20 +78,24 @@ def tile_attend_headwrite_kernel(tc, emb_words, emb_scales, wv, old, retain, off
             for g in range(2)
         ]
         dealt = [g[:].rearrange("p j m t -> p m j t") for g in grouped]
+        nc.vector.tensor_copy(dealt[0][:, :, :, 0:2], w_by_col[:, :, 0:2, 0:2])
+        for cols in (slice(0, P // 2), slice(P // 2, P)):
+            nc.vector.tensor_copy(dealt[0][:, cols, :, 2:4], w_by_col[:, cols, 0:2, 2:4])
         for rows in (slice(0, 2), slice(2, 4)):
-            nc.vector.tensor_copy(dealt[0][:, :, :, rows], w_by_col[:, :, 0:2, rows])
             nc.scalar.activation(dealt[1][:, :, :, rows], w_by_col[:, :, 2:4, rows], COPY)
 
         w_scales = keep.tile([P, E], U8, name="w_scales", align_bytes=64)
         codes = []
 
-        def quantise(g, at):
+        def quantise(g, at, starts, width):
             codes.append(laid.tile([P, 2 * P], U32, name="codes%d" % g, offset=at, align_bytes=64))
-            nc.vector.quantize_mx(
-                out=codes[g][:].bitcast(FP8X4),
-                scales=w_scales[:, 2 * g * P : 2 * (g + 1) * P],
-                in_=grouped[g][:].rearrange("p j m t -> p (j m t)"),
-            )
+            flat = grouped[g][:].rearrange("p j m t -> p (j m t)")
+            for c in starts:
+                nc.vector.quantize_mx(
+                    out=codes[g][:, c : c + width].bitcast(FP8X4),
+                    scales=w_scales[:, 2 * g * P + c : 2 * g * P + c + width],
+                    in_=flat[:, PACK * c : PACK * (c + width)],
+                )
 
         def project(j, cuts, acc):
             first, last = cuts[0], cuts[-1]
@@ -109,7 +113,7 @@ def tile_attend_headwrite_kernel(tc, emb_words, emb_scales, wv, old, retain, off
             nc.scalar.activation(v[:], acc[:, 0 : last - first], COPY)
             return v, place_list[:, first // 16 : last // 16]
 
-        quantise(0, 2 * U)
+        quantise(0, 2 * U, (0, P, P // 2, P + P // 2), P // 2)
         placed.append(keep.tile([P, T], F32, name="placed1", tag="grouped0", align_bytes=64))
         nc.gpsimd.memset(placed[1][:].bitcast(I32), 0)
         for h in range(2):
@@ -117,7 +121,7 @@ def tile_attend_headwrite_kernel(tc, emb_words, emb_scales, wv, old, retain, off
                 got_words[:, 2 * h * HALF : 2 * (h + 1) * HALF].bitcast(U16),
                 words[:].bitcast(U16).indirect(slot_list[:, h * HALF // 16 : (h + 1) * HALF // 16]),
             )
-        quantise(1, 0)
+        quantise(1, 0, (0,), 2 * P)
 
         pieces = [(0, project(0, (0, P), bank[0])), (1, project(1, (0, HALF), bank[1]))]
         pieces.append((0, project(0, (P, HALF, I), bank[2])))

@@ -25,6 +25,8 @@ BANK = 512
 BLOCKS = T // P
 HALF = I // 2
 ROWS = K // 32
+FIRST, STEP = 11, 7
+EARLY = E
 
 
 def tile_attend_headwrite_kernel(tc, emb_words, emb_scales, wv, old, retain, offs, offs2, out):
@@ -40,49 +42,59 @@ def tile_attend_headwrite_kernel(tc, emb_words, emb_scales, wv, old, retain, off
 
         slot_list = keep.tile([P, I // 16], U16, name="slot_list")
         place_list = keep.tile([P, I // 16], U16, name="place_list")
-        scales = keep.tile([P, U], U8, name="scales", tag="scales_old")
-        w_raw = keep.tile([P, PACK * E], F32, name="w_raw")
-        words = laid.tile([P, 2 * U], U8, name="words", offset=0)
-        retain_rows = keep.tile([P, P], F32, name="retain_rows")
+        at_window = 2 * U + 4 * (PACK * E - EARLY) + 8 * P
+        at_scales = at_window + 4 * T
+        scales = laid.tile([P, U], U8, name="scales", offset=at_scales - 64)
+        w_early = keep.tile([P, EARLY], F32, name="w_early")
+        late_bytes = 4 * (PACK * E - EARLY)
+        zeros = laid.tile([P, P], F32, name="zeros", offset=2 * U - 2 * P)
         ident = keep.tile([P, P], F32, name="ident")
 
-        nc.sync.dma_start(scales[P - ROWS : P, :].bitcast(I32), emb_scales[0].bitcast(I32))
-        nc.sync.dma_start(slot_list[:], offs)
+        nc.vector.memset(zeros[:], 0.0)
+        nc.vector.memset(scales[:].bitcast(I32), 0)
+        nc.vector.tensor_copy(ident[:], zeros[:])
+        make_identity(nc, ident[:], nomemset=True)
+        words = laid.tile([P, 2 * U], U8, name="words", offset=0)
+        w_late = laid.tile([P, PACK * E - EARLY], F32, name="w_late", offset=2 * U)
+
         wv_v = wv.rearrange("(p t) e -> p (t e)", t=PACK)
-        for rows in (slice(0, 2 * E), slice(2 * E, 4 * E)):
-            nc.sync.dma_start(w_raw[:, rows], wv_v[:, rows])
-        nc.sync.dma_start(words[:].bitcast(I32), emb_words[0].bitcast(I32))
+        nc.sync.dma_start(w_early[:], wv_v[:, 0:EARLY])
+        nc.sync.dma_start(slot_list[:], offs)
         nc.sync.dma_start(place_list[:], offs2)
+        nc.sync.dma_start(scales[FIRST : FIRST + STEP * ROWS : STEP, :].bitcast(I32), emb_scales[0].bitcast(I32))
+        nc.sync.dma_start(w_late[:], wv_v[:, EARLY : PACK * E])
+        nc.sync.dma_start(words[:].bitcast(I32), emb_words[0].bitcast(I32))
 
         got_words = keep.tile([P, 2 * I], U8, name="got_words", align_bytes=64)
         got_rows = keep.tile([P, I], U8, name="got_rows")
         got_scales = keep.tile([P, I], U8, name="got_scales", align_bytes=64)
         placed = [keep.tile([P, T], F32, name="placed0")]
-        nc.vector.memset(scales[0 : P - ROWS, :].bitcast(I32), 0)
         nc.vector.memset(got_scales[:].bitcast(I32), 0)
-        nc.vector.memset(retain_rows[:], 0.0)
-        nc.sync.dma_start(retain_rows[0:BLOCKS, :], retain.rearrange("o (c p) -> (o c) p", p=P))
         nc.vector.memset(placed[0][:].bitcast(I32), 0)
-        make_identity(nc, ident[:])
 
         nc.vector.tensor_copy(got_rows[:], scales[:].indirect(slot_list[:]))
         for r in range(4):
-            nc.sync.dma_start(got_scales[r:P:32, :].bitcast(I32), got_rows[P - ROWS + r : P : 4, :].bitcast(I32))
-        old_all = keep.tile([P, TILES * T], F32, name="old_all", tag="scales_old")
+            rows = slice(FIRST + STEP * r, FIRST + STEP * (r + 13), 4 * STEP)
+            nc.sync.dma_start(got_scales[r:P:32, :].bitcast(I32), got_rows[rows, :].bitcast(I32))
+        retain_rows = laid.tile([P, P], F32, name="retain_rows", offset=at_scales)
+        nc.gpsimd.memset(retain_rows[0 : P - BLOCKS, :], 0.0)
+        nc.sync.dma_start(retain_rows[P - BLOCKS : P, :], retain.rearrange("o (c p) -> (o c) p", p=P))
+        old_all = laid.tile([P, TILES * T], F32, name="old_all", offset=at_scales + 4 * P)
         for j in range(TILES):
             nc.sync.dma_start(old_all[:, j * T : (j + 1) * T], old_v[:, j, :])
 
-        w_by_col = w_raw[:].rearrange("p (t m j) -> p m j t", t=PACK, j=TILES)
         grouped = [
-            keep.tile([P, 2, P, PACK], BF16, name="grouped%d" % g, tag="grouped%d" % g, align_bytes=64)
-            for g in range(2)
+            laid.tile([P, 2, P, PACK], BF16, name="grouped0", offset=at_scales - 16 * P, align_bytes=64),
+            keep.tile([P, 2, P, PACK], BF16, name="grouped1", tag="grouped1", align_bytes=64),
         ]
         dealt = [g[:].rearrange("p j m t -> p m j t") for g in grouped]
-        nc.vector.tensor_copy(dealt[0][:, :, :, 0:2], w_by_col[:, :, 0:2, 0:2])
+        early = w_early[:].rearrange("p (t m j) -> p m j t", t=1, j=TILES)
+        late = w_late[:].rearrange("p (t m j) -> p m j t", t=PACK - 1, j=TILES)
+        nc.vector.tensor_copy(dealt[0][:, :, :, 0:1], early[:, :, 0:2, :])
         for cols in (slice(0, P // 2), slice(P // 2, P)):
-            nc.vector.tensor_copy(dealt[0][:, cols, :, 2:4], w_by_col[:, cols, 0:2, 2:4])
-        for rows in (slice(0, 2), slice(2, 4)):
-            nc.scalar.activation(dealt[1][:, :, :, rows], w_by_col[:, :, 2:4, rows], COPY)
+            nc.vector.tensor_copy(dealt[0][:, cols, :, 1:PACK], late[:, cols, 0:2, :])
+        nc.scalar.activation(dealt[1][:, :, :, 0:1], early[:, :, 2:4, :], COPY)
+        nc.scalar.activation(dealt[1][:, :, :, 1:PACK], late[:, :, 2:4, :], COPY)
 
         w_scales = keep.tile([P, E], U8, name="w_scales", align_bytes=64)
         codes = []
@@ -113,8 +125,8 @@ def tile_attend_headwrite_kernel(tc, emb_words, emb_scales, wv, old, retain, off
             nc.scalar.activation(v[:], acc[:, 0 : last - first], COPY)
             return v, place_list[:, first // 16 : last // 16]
 
-        quantise(0, 2 * U, (0, P, P // 2, P + P // 2), P // 2)
-        placed.append(keep.tile([P, T], F32, name="placed1", tag="grouped0", align_bytes=64))
+        quantise(0, 2 * U + late_bytes, (0, P, P // 2, P + P // 2), P // 2)
+        placed.append(laid.tile([P, T], F32, name="placed1", offset=at_window))
         nc.gpsimd.memset(placed[1][:].bitcast(I32), 0)
         for h in range(2):
             nc.vector.tensor_copy(
@@ -129,7 +141,7 @@ def tile_attend_headwrite_kernel(tc, emb_words, emb_scales, wv, old, retain, off
 
         nc.tensor.transpose(bank[0][:, 0:P], retain_rows[:], ident[:])
         retain_cols = keep.tile([P, BLOCKS], F32, name="retain_cols")
-        nc.scalar.activation(retain_cols[:], bank[0][:, 0:BLOCKS], COPY)
+        nc.scalar.activation(retain_cols[:], bank[0][:, P - BLOCKS : P], COPY)
         retain_all = keep.tile([P, T], F32, name="retain_all")
         for b in range(T // BANK):
             for c in range(BANK // P):

@@ -26,7 +26,6 @@ BLOCKS = T // P
 HALF = I // 2
 ROWS = K // 32
 FIRST, STEP = 11, 7
-EARLY = E
 
 
 def tile_attend_headwrite_kernel(tc, emb_words, emb_scales, wv, old, retain, offs, offs2, out):
@@ -42,28 +41,30 @@ def tile_attend_headwrite_kernel(tc, emb_words, emb_scales, wv, old, retain, off
 
         slot_list = keep.tile([P, I // 16], U16, name="slot_list")
         place_list = keep.tile([P, I // 16], U16, name="place_list")
-        at_window = 2 * U + 4 * (PACK * E - EARLY) + 8 * P
-        at_scales = at_window + 4 * T
-        scales = laid.tile([P, U], U8, name="scales", offset=at_scales - 64)
-        w_early = keep.tile([P, EARLY], F32, name="w_early")
-        late_bytes = 4 * (PACK * E - EARLY)
+        scales = keep.tile([P, U], U8, name="scales", tag="scales_old")
+        w_low = keep.tile([P, 2, E // 2], F32, name="w_low")
         zeros = laid.tile([P, P], F32, name="zeros", offset=2 * U - 2 * P)
+        retain_rows = keep.tile([P, P], F32, name="retain_rows")
         ident = keep.tile([P, P], F32, name="ident")
 
         nc.vector.memset(zeros[:], 0.0)
         nc.vector.memset(scales[:].bitcast(I32), 0)
         nc.vector.tensor_copy(ident[:], zeros[:])
+        nc.vector.memset(retain_rows[:], 0.0)
         make_identity(nc, ident[:], nomemset=True)
         words = laid.tile([P, 2 * U], U8, name="words", offset=0)
-        w_late = laid.tile([P, PACK * E - EARLY], F32, name="w_late", offset=2 * U)
+        w_held = laid.tile([P, 3 * E], F32, name="w_held", offset=2 * U)
+        w_high = w_held[:, 0:E].rearrange("p (t e) -> p t e", t=2)
 
-        wv_v = wv.rearrange("(p t) e -> p (t e)", t=PACK)
-        nc.sync.dma_start(w_early[:], wv_v[:, 0:EARLY])
+        wv_v = wv.rearrange("(p t) e -> p t e", t=PACK)
+        nc.sync.dma_start(w_low[:], wv_v[:, 0:2, 0 : E // 2])
         nc.sync.dma_start(slot_list[:], offs)
         nc.sync.dma_start(place_list[:], offs2)
         nc.sync.dma_start(scales[FIRST : FIRST + STEP * ROWS : STEP, :].bitcast(I32), emb_scales[0].bitcast(I32))
-        nc.sync.dma_start(w_late[:], wv_v[:, EARLY : PACK * E])
+        nc.sync.dma_start(w_high, wv_v[:, 0:2, E // 2 : E])
+        nc.sync.dma_start(w_held[:, E : 3 * E], wv_v[:, 2:4, :].rearrange("p t e -> p (t e)"))
         nc.sync.dma_start(words[:].bitcast(I32), emb_words[0].bitcast(I32))
+        nc.sync.dma_start(retain_rows[0:BLOCKS, :], retain.rearrange("o (c p) -> (o c) p", p=P))
 
         got_words = keep.tile([P, 2 * I], U8, name="got_words", align_bytes=64)
         got_rows = keep.tile([P, I], U8, name="got_rows")
@@ -74,27 +75,25 @@ def tile_attend_headwrite_kernel(tc, emb_words, emb_scales, wv, old, retain, off
 
         nc.vector.tensor_copy(got_rows[:], scales[:].indirect(slot_list[:]))
         for r in range(4):
-            rows = slice(FIRST + STEP * r, FIRST + STEP * (r + 13), 4 * STEP)
-            nc.sync.dma_start(got_scales[r:P:32, :].bitcast(I32), got_rows[rows, :].bitcast(I32))
-        retain_rows = laid.tile([P, P], F32, name="retain_rows", offset=at_scales)
-        nc.gpsimd.memset(retain_rows[0 : P - BLOCKS, :], 0.0)
-        nc.sync.dma_start(retain_rows[P - BLOCKS : P, :], retain.rearrange("o (c p) -> (o c) p", p=P))
-        old_all = laid.tile([P, TILES * T], F32, name="old_all", offset=at_scales + 4 * P)
+            nc.sync.dma_start(got_scales[r:P:32, :].bitcast(I32), got_rows[FIRST + STEP * r : FIRST + STEP * (r + 13) : 4 * STEP, :].bitcast(I32))
+        old_all = keep.tile([P, TILES * T], F32, name="old_all", tag="scales_old")
         for j in range(TILES):
             nc.sync.dma_start(old_all[:, j * T : (j + 1) * T], old_v[:, j, :])
 
         grouped = [
-            laid.tile([P, 2, P, PACK], BF16, name="grouped0", offset=at_scales - 16 * P, align_bytes=64),
-            keep.tile([P, 2, P, PACK], BF16, name="grouped1", tag="grouped1", align_bytes=64),
+            keep.tile([P, 2, P, PACK], BF16, name="grouped%d" % g, tag="grouped%d" % g, align_bytes=64)
+            for g in range(2)
         ]
         dealt = [g[:].rearrange("p j m t -> p m j t") for g in grouped]
-        early = w_early[:].rearrange("p (t m j) -> p m j t", t=1, j=TILES)
-        late = w_late[:].rearrange("p (t m j) -> p m j t", t=PACK - 1, j=TILES)
-        nc.vector.tensor_copy(dealt[0][:, :, :, 0:1], early[:, :, 0:2, :])
-        for cols in (slice(0, P // 2), slice(P // 2, P)):
-            nc.vector.tensor_copy(dealt[0][:, cols, :, 1:PACK], late[:, cols, 0:2, :])
-        nc.scalar.activation(dealt[1][:, :, :, 0:1], early[:, :, 2:4, :], COPY)
-        nc.scalar.activation(dealt[1][:, :, :, 1:PACK], late[:, :, 2:4, :], COPY)
+        halves = (slice(0, P // 2), slice(P // 2, P))
+        for cols, src in zip(halves, (w_low[:], w_high)):
+            by_col = src.rearrange("p t (m j) -> p m j t", j=TILES)
+            nc.vector.tensor_copy(dealt[0][:, cols, :, 0:2], by_col[:, :, 0:2, :])
+            nc.scalar.activation(dealt[1][:, cols, :, 0:2], by_col[:, :, 2:4, :], COPY)
+        by_col = w_held[:, E : 3 * E].rearrange("p (t m j) -> p m j t", t=2, j=TILES)
+        for cols in halves:
+            nc.vector.tensor_copy(dealt[0][:, cols, :, 2:4], by_col[:, cols, 0:2, :])
+        nc.scalar.activation(dealt[1][:, :, :, 2:4], by_col[:, :, 2:4, :], COPY)
 
         w_scales = keep.tile([P, E], U8, name="w_scales", align_bytes=64)
         codes = []
@@ -125,8 +124,8 @@ def tile_attend_headwrite_kernel(tc, emb_words, emb_scales, wv, old, retain, off
             nc.scalar.activation(v[:], acc[:, 0 : last - first], COPY)
             return v, place_list[:, first // 16 : last // 16]
 
-        quantise(0, 2 * U + late_bytes, (0, P, P // 2, P + P // 2), P // 2)
-        placed.append(laid.tile([P, T], F32, name="placed1", offset=at_window))
+        quantise(0, 2 * U + 12 * E, (0, P, P // 2, P + P // 2), P // 2)
+        placed.append(keep.tile([P, T], F32, name="placed1", tag="grouped0", align_bytes=64))
         nc.gpsimd.memset(placed[1][:].bitcast(I32), 0)
         for h in range(2):
             nc.vector.tensor_copy(
@@ -139,9 +138,9 @@ def tile_attend_headwrite_kernel(tc, emb_words, emb_scales, wv, old, retain, off
         pieces.append((0, project(0, (P, HALF, I), bank[2])))
         pieces.append((1, project(1, (HALF, I), bank[3])))
 
-        nc.tensor.transpose(bank[0][:, 0:P], retain_rows[:], ident[:])
+        nc.tensor.transpose(bank[4][:, 0:P], retain_rows[:], ident[:])
         retain_cols = keep.tile([P, BLOCKS], F32, name="retain_cols")
-        nc.scalar.activation(retain_cols[:], bank[0][:, P - BLOCKS : P], COPY)
+        nc.scalar.activation(retain_cols[:], bank[4][:, 0:BLOCKS], COPY)
         retain_all = keep.tile([P, T], F32, name="retain_all")
         for b in range(T // BANK):
             for c in range(BANK // P):

@@ -42,36 +42,31 @@ def tile_attend_headwrite_kernel(tc, emb_words, emb_scales, wv, old, retain, off
         slot_list = keep.tile([P, I // 16], U16, name="slot_list")
         place_list = keep.tile([P, I // 16], U16, name="place_list")
         scales = keep.tile([P, U], U8, name="scales", tag="scales_old")
-        w_low = keep.tile([P, 2, E // 2], F32, name="w_low")
-        zeros = laid.tile([P, P], F32, name="zeros", offset=2 * U - 2 * P)
+        w_raw = keep.tile([P, PACK, E], F32, name="w_raw")
+        words = laid.tile([P, 2 * U], U8, name="words", offset=0)
         retain_rows = keep.tile([P, P], F32, name="retain_rows")
         ident = keep.tile([P, P], F32, name="ident")
 
-        nc.vector.memset(zeros[:], 0.0)
         nc.vector.memset(scales[:].bitcast(I32), 0)
-        nc.vector.tensor_copy(ident[:], zeros[:])
-        nc.vector.memset(retain_rows[:], 0.0)
-        make_identity(nc, ident[:], nomemset=True)
-        words = laid.tile([P, 2 * U], U8, name="words", offset=0)
-        w_held = laid.tile([P, 3 * E], F32, name="w_held", offset=2 * U)
-        w_high = w_held[:, 0:E].rearrange("p (t e) -> p t e", t=2)
-
         wv_v = wv.rearrange("(p t) e -> p t e", t=PACK)
-        nc.sync.dma_start(w_low[:], wv_v[:, 0:2, 0 : E // 2])
+        for c in range(0, E // 2, P):
+            nc.sync.dma_start(w_raw[:, 0:2, c : c + P], wv_v[:, 0:2, c : c + P])
         nc.sync.dma_start(slot_list[:], offs)
-        nc.sync.dma_start(place_list[:], offs2)
         nc.sync.dma_start(scales[FIRST : FIRST + STEP * ROWS : STEP, :].bitcast(I32), emb_scales[0].bitcast(I32))
-        nc.sync.dma_start(w_high, wv_v[:, 0:2, E // 2 : E])
-        nc.sync.dma_start(w_held[:, E : 3 * E], wv_v[:, 2:4, :].rearrange("p t e -> p (t e)"))
+        nc.sync.dma_start(w_raw[:, 0:2, E // 2 : E], wv_v[:, 0:2, E // 2 : E])
+        nc.sync.dma_start(w_raw[:, 2:4, :], wv_v[:, 2:4, :])
         nc.sync.dma_start(words[:].bitcast(I32), emb_words[0].bitcast(I32))
-        nc.sync.dma_start(retain_rows[0:BLOCKS, :], retain.rearrange("o (c p) -> (o c) p", p=P))
+        nc.sync.dma_start(place_list[:], offs2)
 
         got_words = keep.tile([P, 2 * I], U8, name="got_words", align_bytes=64)
         got_rows = keep.tile([P, I], U8, name="got_rows")
         got_scales = keep.tile([P, I], U8, name="got_scales", align_bytes=64)
         placed = [keep.tile([P, T], F32, name="placed0")]
         nc.vector.memset(got_scales[:].bitcast(I32), 0)
+        nc.vector.memset(retain_rows[:], 0.0)
+        nc.sync.dma_start(retain_rows[0:BLOCKS, :], retain.rearrange("o (c p) -> (o c) p", p=P))
         nc.vector.memset(placed[0][:].bitcast(I32), 0)
+        make_identity(nc, ident[:])
 
         nc.vector.tensor_copy(got_rows[:], scales[:].indirect(slot_list[:]))
         for r in range(4):
@@ -85,15 +80,13 @@ def tile_attend_headwrite_kernel(tc, emb_words, emb_scales, wv, old, retain, off
             for g in range(2)
         ]
         dealt = [g[:].rearrange("p j m t -> p m j t") for g in grouped]
-        halves = (slice(0, P // 2), slice(P // 2, P))
-        for cols, src in zip(halves, (w_low[:], w_high)):
-            by_col = src.rearrange("p t (m j) -> p m j t", j=TILES)
-            nc.vector.tensor_copy(dealt[0][:, cols, :, 0:2], by_col[:, :, 0:2, :])
-            nc.scalar.activation(dealt[1][:, cols, :, 0:2], by_col[:, :, 2:4, :], COPY)
-        by_col = w_held[:, E : 3 * E].rearrange("p (t m j) -> p m j t", t=2, j=TILES)
-        for cols in halves:
-            nc.vector.tensor_copy(dealt[0][:, cols, :, 2:4], by_col[:, cols, 0:2, :])
-        nc.scalar.activation(dealt[1][:, :, :, 2:4], by_col[:, :, 2:4, :], COPY)
+        w_by_col = w_raw[:].rearrange("p t (m j) -> p m j t", j=TILES)
+        nc.vector.tensor_copy(dealt[0][:, :, :, 0:2], w_by_col[:, :, 0:2, 0:2])
+        for cols in (slice(0, P // 2), slice(P // 2, P)):
+            nc.vector.tensor_copy(dealt[0][:, cols, :, 2:4], w_by_col[:, cols, 0:2, 2:4])
+        for cols in (slice(0, P // 4), slice(P // 4, P)):
+            nc.scalar.activation(dealt[1][:, cols, :, 0:2], w_by_col[:, cols, 2:4, 0:2], COPY)
+        nc.scalar.activation(dealt[1][:, :, :, 2:4], w_by_col[:, :, 2:4, 2:4], COPY)
 
         w_scales = keep.tile([P, E], U8, name="w_scales", align_bytes=64)
         codes = []
@@ -124,7 +117,7 @@ def tile_attend_headwrite_kernel(tc, emb_words, emb_scales, wv, old, retain, off
             nc.scalar.activation(v[:], acc[:, 0 : last - first], COPY)
             return v, place_list[:, first // 16 : last // 16]
 
-        quantise(0, 2 * U + 12 * E, (0, P, P // 2, P + P // 2), P // 2)
+        quantise(0, 2 * U, (0, P, P // 2, P + P // 2), P // 2)
         placed.append(keep.tile([P, T], F32, name="placed1", tag="grouped0", align_bytes=64))
         nc.gpsimd.memset(placed[1][:].bitcast(I32), 0)
         for h in range(2):

@@ -42,19 +42,19 @@ def tile_attend_headwrite_kernel(tc, emb_words, emb_scales, wv, old, retain, off
         slot_list = keep.tile([P, I // 16], U16, name="slot_list")
         place_list = keep.tile([P, I // 16], U16, name="place_list")
         scales = keep.tile([P, U], U8, name="scales", tag="scales_old")
-        w_raw = keep.tile([P, PACK, E], F32, name="w_raw")
+        w_raw = keep.tile([P, PACK * E], F32, name="w_raw")
         words = laid.tile([P, 2 * U], U8, name="words", offset=0)
         retain_rows = keep.tile([P, P], F32, name="retain_rows")
         ident = keep.tile([P, P], F32, name="ident")
 
         nc.vector.memset(scales[:].bitcast(I32), 0)
-        wv_v = wv.rearrange("(p t) e -> p t e", t=PACK)
-        for c in range(0, E // 2, P):
-            nc.sync.dma_start(w_raw[:, 0:2, c : c + P], wv_v[:, 0:2, c : c + P])
+        nc.vector.memset(ident[:], 0.0)
+        wv_v = wv.rearrange("(p t) e -> p (t e)", t=PACK)
+        nc.sync.dma_start(w_raw[:, 0:E], wv_v[:, 0:E])
         nc.sync.dma_start(slot_list[:], offs)
         nc.sync.dma_start(scales[FIRST : FIRST + STEP * ROWS : STEP, :].bitcast(I32), emb_scales[0].bitcast(I32))
-        nc.sync.dma_start(w_raw[:, 0:2, E // 2 : E], wv_v[:, 0:2, E // 2 : E])
-        nc.sync.dma_start(w_raw[:, 2:4, :], wv_v[:, 2:4, :])
+        nc.sync.dma_start(w_raw[:, E : 2 * E], wv_v[:, E : 2 * E])
+        nc.sync.dma_start(w_raw[:, 2 * E : 4 * E], wv_v[:, 2 * E : 4 * E])
         nc.sync.dma_start(words[:].bitcast(I32), emb_words[0].bitcast(I32))
         nc.sync.dma_start(place_list[:], offs2)
 
@@ -66,7 +66,7 @@ def tile_attend_headwrite_kernel(tc, emb_words, emb_scales, wv, old, retain, off
         nc.vector.memset(retain_rows[:], 0.0)
         nc.sync.dma_start(retain_rows[0:BLOCKS, :], retain.rearrange("o (c p) -> (o c) p", p=P))
         nc.vector.memset(placed[0][:].bitcast(I32), 0)
-        make_identity(nc, ident[:])
+        make_identity(nc, ident[:], nomemset=True)
 
         nc.vector.tensor_copy(got_rows[:], scales[:].indirect(slot_list[:]))
         for r in range(4):
@@ -80,13 +80,12 @@ def tile_attend_headwrite_kernel(tc, emb_words, emb_scales, wv, old, retain, off
             for g in range(2)
         ]
         dealt = [g[:].rearrange("p j m t -> p m j t") for g in grouped]
-        w_by_col = w_raw[:].rearrange("p t (m j) -> p m j t", j=TILES)
+        w_by_col = w_raw[:].rearrange("p (t m j) -> p m j t", t=PACK, j=TILES)
         nc.vector.tensor_copy(dealt[0][:, :, :, 0:2], w_by_col[:, :, 0:2, 0:2])
         for cols in (slice(0, P // 2), slice(P // 2, P)):
             nc.vector.tensor_copy(dealt[0][:, cols, :, 2:4], w_by_col[:, cols, 0:2, 2:4])
-        for cols in (slice(0, P // 4), slice(P // 4, P)):
-            nc.scalar.activation(dealt[1][:, cols, :, 0:2], w_by_col[:, cols, 2:4, 0:2], COPY)
-        nc.scalar.activation(dealt[1][:, :, :, 2:4], w_by_col[:, :, 2:4, 2:4], COPY)
+        for rows in (slice(0, 1), slice(1, 2), slice(2, 4)):
+            nc.scalar.activation(dealt[1][:, :, :, rows], w_by_col[:, :, 2:4, rows], COPY)
 
         w_scales = keep.tile([P, E], U8, name="w_scales", align_bytes=64)
         codes = []

from contextlib import ExitStack

import concourse.mybir as mybir
from concourse.masks import make_identity

K, U, I, T, E = 512, 2048, 512, 1024, 512
FLOPS = 2 * K * E * I

F32 = mybir.dt.float32
BF16 = mybir.dt.bfloat16
I32 = mybir.dt.int32
U32 = mybir.dt.uint32
U16 = mybir.dt.uint16
U8 = mybir.dt.uint8
FP8X4 = mybir.dt.float8_e4m3fn_x4
FP4X4 = mybir.dt.float4_e2m1fn_x4
COPY = mybir.ActivationFunctionType.Copy
ADD = mybir.AluOpType.add
MULT = mybir.AluOpType.mult

P = 128
PACK = 4
TILES = E // P
BANK = 512
BLOCKS = T // P
HALF = I // 2
ROWS = K // 32
FIRST, STEP = 11, 7


def tile_attend_headwrite_kernel(tc, emb_words, emb_scales, wv, old, retain, offs, offs2, out):
    nc = tc.nc
    with ExitStack() as ctx:
        keep = ctx.enter_context(tc.tile_pool(name="keep", bufs=1))
        laid = ctx.enter_context(tc.tile_pool(name="laid", bufs=1))
        psum = ctx.enter_context(tc.psum_pool(name="psum", bufs=1))
        bank = [psum.tile([P, BANK], F32, name="bank%d" % b) for b in range(8)]

        old_v = old.rearrange("(p j) t -> p j t", j=TILES)
        out_v = out.rearrange("(p j) t -> p j t", j=TILES)

        slot_list = keep.tile([P, I // 16], U16, name="slot_list")
        place_list = keep.tile([P, I // 16], U16, name="place_list")
        scales = keep.tile([P, U], U8, name="scales", tag="scales_old")
        w_raw = keep.tile([P, PACK * E], F32, name="w_raw")
        words = laid.tile([P, 2 * U], U8, name="words", offset=0)
        retain_rows = keep.tile([P, P], F32, name="retain_rows")
        ident = keep.tile([P, P], F32, name="ident")

        nc.vector.memset(scales[:].bitcast(I32), 0)
        nc.vector.memset(ident[:], 0.0)
        wv_v = wv.rearrange("(p t) e -> p (t e)", t=PACK)
        nc.sync.dma_start(w_raw[:, 0:E], wv_v[:, 0:E])
        nc.sync.dma_start(slot_list[:], offs)
        nc.sync.dma_start(scales[FIRST : FIRST + STEP * ROWS : STEP, :].bitcast(I32), emb_scales[0].bitcast(I32))
        nc.sync.dma_start(w_raw[:, E : 2 * E], wv_v[:, E : 2 * E])
        nc.sync.dma_start(w_raw[:, 2 * E : 4 * E], wv_v[:, 2 * E : 4 * E])
        nc.sync.dma_start(words[:].bitcast(I32), emb_words[0].bitcast(I32))
        nc.sync.dma_start(place_list[:], offs2)

        got_words = keep.tile([P, 2 * I], U8, name="got_words", align_bytes=64)
        got_rows = keep.tile([P, I], U8, name="got_rows")
        got_scales = keep.tile([P, I], U8, name="got_scales", align_bytes=64)
        placed = [keep.tile([P, T], F32, name="placed0")]
        nc.vector.memset(got_scales[:].bitcast(I32), 0)
        nc.vector.memset(retain_rows[:], 0.0)
        nc.sync.dma_start(retain_rows[0:BLOCKS, :], retain.rearrange("o (c p) -> (o c) p", p=P))
        nc.vector.memset(placed[0][:].bitcast(I32), 0)
        make_identity(nc, ident[:], nomemset=True)

        nc.vector.tensor_copy(got_rows[:], scales[:].indirect(slot_list[:]))
        for r in range(4):
            nc.sync.dma_start(got_scales[r:P:32, :].bitcast(I32), got_rows[FIRST + STEP * r : FIRST + STEP * (r + 13) : 4 * STEP, :].bitcast(I32))
        old_all = keep.tile([P, TILES * T], F32, name="old_all", tag="scales_old")
        for j in range(TILES):
            nc.sync.dma_start(old_all[:, j * T : (j + 1) * T], old_v[:, j, :])

        grouped = [
            keep.tile([P, 2, P, PACK], BF16, name="grouped%d" % g, tag="grouped%d" % g, align_bytes=64)
            for g in range(2)
        ]
        dealt = [g[:].rearrange("p j m t -> p m j t") for g in grouped]
        w_by_col = w_raw[:].rearrange("p (t m j) -> p m j t", t=PACK, j=TILES)
        nc.vector.tensor_copy(dealt[0][:, :, :, 0:2], w_by_col[:, :, 0:2, 0:2])
        for cols in (slice(0, P // 2), slice(P // 2, P)):
            nc.vector.tensor_copy(dealt[0][:, cols, :, 2:4], w_by_col[:, cols, 0:2, 2:4])
        for rows in (slice(0, 1), slice(1, 2), slice(2, 4)):
            nc.scalar.activation(dealt[1][:, :, :, rows], w_by_col[:, :, 2:4, rows], COPY)

        w_scales = keep.tile([P, E], U8, name="w_scales", align_bytes=64)
        codes = []

        def quantise(g, at, starts, width):
            codes.append(laid.tile([P, 2 * P], U32, name="codes%d" % g, offset=at, align_bytes=64))
            flat = grouped[g][:].rearrange("p j m t -> p (j m t)")
            for c in starts:
                nc.vector.quantize_mx(
                    out=codes[g][:, c : c + width].bitcast(FP8X4),
                    scales=w_scales[:, 2 * g * P + c : 2 * g * P + c + width],
                    in_=flat[:, PACK * c : PACK * (c + width)],
                )

        def project(j, cuts, acc):
            first, last = cuts[0], cuts[-1]
            for i0, i1 in zip(cuts, cuts[1:]):
                nc.tensor.matmul_mx(
                    out=acc[:, i0 - first : i1 - first],
                    lhsT=codes[j // 2][:, j % 2 * P : (j % 2 + 1) * P].bitcast(FP8X4),
                    lhsT_scale=w_scales[:, j * P : (j + 1) * P],
                    rhs=got_words[:, 2 * i0 : 2 * i1].bitcast(FP4X4),
                    rhs_scale=got_scales[:, i0:i1],
                    start=True,
                    stop=True,
                )
            v = keep.tile([P, last - first], F32, name="v%d_%d" % (j, first))
            nc.scalar.activation(v[:], acc[:, 0 : last - first], COPY)
            return v, place_list[:, first // 16 : last // 16]

        quantise(0, 2 * U, (0, P, P // 2, P + P // 2), P // 2)
        placed.append(keep.tile([P, T], F32, name="placed1", tag="grouped0", align_bytes=64))
        nc.gpsimd.memset(placed[1][:].bitcast(I32), 0)
        for h in range(2):
            nc.vector.tensor_copy(
                got_words[:, 2 * h * HALF : 2 * (h + 1) * HALF].bitcast(U16),
                words[:].bitcast(U16).indirect(slot_list[:, h * HALF // 16 : (h + 1) * HALF // 16]),
            )
        quantise(1, 0, (0,), 2 * P)

        pieces = [(0, project(0, (0, P), bank[0])), (1, project(1, (0, HALF), bank[1]))]
        pieces.append((0, project(0, (P, HALF, I), bank[2])))
        pieces.append((1, project(1, (HALF, I), bank[3])))

        nc.tensor.transpose(bank[4][:, 0:P], retain_rows[:], ident[:])
        retain_cols = keep.tile([P, BLOCKS], F32, name="retain_cols")
        nc.scalar.activation(retain_cols[:], bank[4][:, 0:BLOCKS], COPY)
        retain_all = keep.tile([P, T], F32, name="retain_all")
        for b in range(T // BANK):
            for c in range(BANK // P):
                col = b * (BANK // P) + c
                nc.tensor.transpose(
                    bank[b][:, c * P : (c + 1) * P], retain_cols[:, col : col + 1].to_broadcast([P, P]), ident[:]
                )
            nc.scalar.activation(retain_all[:, b * BANK : (b + 1) * BANK], bank[b][:], COPY)

        pieces.append((2, project(2, (0, I), bank[5])))

        placed.append(keep.tile([P, T], F32, name="placed2", tag="grouped1", align_bytes=64))
        nc.gpsimd.memset(placed[2][:].bitcast(I32), 0)
        for b in range(T // BANK):
            cols = slice(b * BANK, (b + 1) * BANK)
            nc.gpsimd.tensor_tensor(old_all[:, cols], old_all[:, cols], retain_all[:, cols], MULT)

        for step in range(T // BANK, TILES * T // BANK):
            j, b = divmod(step, T // BANK)
            turn = bank[step % 3]
            back = bank[6 + b] if j == TILES - 1 else bank[3 + step % 2]
            turned = keep.tile([P, BANK], F32, name="turned%d" % step)
            for cc in range(4):
                at = step * BANK + cc * P
                nc.tensor.transpose(turn[:, cc * P : (cc + 1) * P], old_all[:, at : at + P], ident[:])
            for cc in range(4):
                c = 4 * b + cc
                cols = slice(cc * P, (cc + 1) * P)
                nc.scalar.activation(turned[:, cols], turn[:, cols], COPY, scale=retain_cols[:, c : c + 1])
            for cc in range(4):
                cols = slice(cc * P, (cc + 1) * P)
                nc.tensor.transpose(back[:, cols], turned[:, cols], ident[:])
            if j < TILES - 1:
                nc.scalar.activation(old_all[:, step * BANK : (step + 1) * BANK], back[:], COPY)
            if (j, b) == (1, 1):
                pieces.append((3, project(3, (0, I), bank[5])))
        kept = [old_all[:, j * T : (j + 1) * T] for j in range(TILES - 1)]

        for j, (v, places) in pieces[:-1]:
            nc.vector.tensor_copy(placed[j][:].indirect(places), v[:])
        for j in range(TILES - 1):
            parts = 2 if j == TILES - 2 else 1
            for b in range(parts):
                cols = slice(b * T // parts, (b + 1) * T // parts)
                nc.gpsimd.tensor_tensor(kept[j][:, cols], kept[j][:, cols], placed[j][:, cols], ADD)
                nc.sync.dma_start(out_v[:, j, cols], kept[j][:, cols])

        v, places = pieces[-1][1]
        nc.vector.tensor_copy(placed[0][:].indirect(places), v[:])
        last = keep.tile([P, T], F32, name="last", tag="grouped1", align_bytes=64)
        for q in range(4):
            cols = slice(q * HALF, (q + 1) * HALF)
            in_bank = slice(q % 2 * HALF, (q % 2 + 1) * HALF)
            nc.vector.tensor_tensor(last[:, cols], bank[6 + q // 2][:, in_bank], placed[0][:, cols], ADD)
            nc.sync.dma_start(out_v[:, 3, cols], last[:, cols])
